import numpy as np
import ml_dtypes


def mxq(x, axis, fmt="e4m3"):
    dtype, down = {"e4m3": (ml_dtypes.float8_e4m3fn, 7), "e5m2": (ml_dtypes.float8_e5m2, 14)}[fmt]
    v = np.moveaxis(np.asarray(x, np.float32).astype(ml_dtypes.bfloat16).astype(np.float64), axis, -1)
    blocks = v.reshape(v.shape[:-1] + (-1, 32))
    amax = np.abs(blocks).max(-1, keepdims=True)
    byte = np.maximum(np.where(amax > 0, np.frexp(amax)[1] - 1 + 127, 0) - down, 1)
    scale = np.exp2(byte - 127.0)
    codes = (blocks / scale).astype(np.float32).astype(dtype).astype(np.float64)
    return np.moveaxis((codes * scale).reshape(v.shape), -1, axis)


WIDE = False


def mx_kscale(k):
    if not WIDE:
        return np.ones(k)
    levels = np.array([10, -10, 5, -5, 0])
    if k % 512:
        return np.exp2(np.random.permutation(np.resize(levels, k // 32))).repeat(32)
    a = np.empty((k // 512, 16))
    for p in range(k // 512):
        a[p, :8] = np.random.permutation(np.resize(levels, 8))
        for g in range(8):
            far = levels[np.abs(levels - a[p, g]) >= 10]
            a[p, g + 8] = far[np.random.randint(len(far))]
    return np.exp2(a.ravel()).repeat(32)


def f64(x):
    return np.asarray(x).astype(np.float64)


def striped8(idx):
    return np.asarray(idx).reshape(8, -1, 16).transpose(0, 2, 1).reshape(128, -1).astype(np.uint16)


def unstriped8(offs):
    return offs.reshape(8, 16, -1).transpose(0, 2, 1).reshape(8, -1).astype(np.int64)


def pick8(x, idx, run):
    r = np.arange(len(x))
    return x[r[:, None], idx[r % (8 * run) // run]]


E2M1 = np.array([0.0, 0.5, 1.0, 1.5, 2.0, 3.0, 4.0, 6.0, -0.0, -0.5, -1.0, -1.5, -2.0, -3.0, -4.0, -6.0])


def pack_weight(w, fmt):
    k, n = w.shape
    w = f64(np.asarray(w, np.float32).astype(ml_dtypes.bfloat16)).reshape(k // 32, 32, n)
    amax = np.abs(w).max(1)
    if fmt == "e4m3":
        byte = np.frexp(amax)[1] - 1 + 127 - 7
    else:
        mant, ex = np.frexp(amax / 6.0)
        byte = np.where(mant > 0.5, ex, ex - 1) + 127
    byte = np.clip(np.where(amax > 0, byte, 1), 1, 254)
    scaled = (w * np.exp2(127.0 - byte)[:, None, :]).reshape(k, n).astype(np.float32)
    by_word = np.ascontiguousarray(scaled.reshape(k // 512, 128, 4, n).transpose(0, 1, 3, 2))
    if fmt == "e4m3":
        words = by_word.astype(ml_dtypes.float8_e4m3fn).view(np.uint8)
    else:
        c = by_word.astype(ml_dtypes.float4_e2m1fn).view(np.uint8) & 0xF
        words = (c[..., 0::2] | (c[..., 1::2] << 4)).reshape(k // 512, 128, 2 * n)
    return np.ascontiguousarray(words), np.ascontiguousarray(byte.astype(np.uint8).reshape(k // 512, 16, n))


def unpack_weight(words, scales, fmt):
    g, _, n = scales.shape
    words = np.ascontiguousarray(words).reshape(g, 128, n, -1)
    if fmt == "e4m3":
        vals = words.view(ml_dtypes.float8_e4m3fn).astype(np.float64)
    else:
        nib = np.empty((g, 128, n, 4), np.uint8)
        nib[..., 0::2] = words & 0xF
        nib[..., 1::2] = words >> 4
        vals = E2M1[nib]
    vals = vals * np.repeat(np.exp2(scales.astype(np.float64) - 127.0), 8, axis=1)[..., None]
    return vals.transpose(0, 1, 3, 2).reshape(g * 512, n)


D, C, I, Q, E = 512, 1024, 512, 128, 512


def setup_inputs():
    n = np.random.standard_normal
    idx = np.stack([np.random.randint(0, C, I) for _ in range(8)])
    fd = mx_kscale(D)
    fi = mx_kscale(I)
    bookp = pack_weight(n((D, C)) / fd[:, None], "e4m3")
    return {
        "book_words": bookp[0],
        "book_scales": bookp[1],
        "query": (n((D, Q)) * 0.2 / np.sqrt(D) * fd[:, None]).astype(np.float32),
        "size": (np.random.uniform(0.5, 2.0, (1, I)) * fi).astype(np.float32),
        "vals": (n((I, E)) / fi[:, None]).astype(np.float32),
        "offs": striped8(idx),
    }


def reference(book_words, book_scales, query, size, vals, offs):
    idx = unstriped8(offs)
    booku = unpack_weight(book_words, book_scales, "e4m3")
    queryq = mxq(f64(query), 0, "e4m3")
    bookidxg = pick8(booku, idx, 64)
    a = queryq.T @ bookidxg
    p = np.exp(a - np.max(a, axis=1, keepdims=True))
    w = p * f64(size) / np.sum(p, axis=1, keepdims=True)
    wt = w.T
    wtq = mxq(wt, 0, "e4m3")
    valsq = mxq(f64(vals), 0, "e4m3")
    o = wtq.T @ valsq
    return o

@@ -1,0 +1,148 @@
+from contextlib import ExitStack
+
+import concourse.mybir as mybir
+from concourse.masks import make_identity
+
+F32 = mybir.dt.float32
+BF16 = mybir.dt.bfloat16
+I32 = mybir.dt.int32
+U32 = mybir.dt.uint32
+U16 = mybir.dt.uint16
+U8 = mybir.dt.uint8
+FP8X4 = mybir.dt.float8_e4m3fn_x4
+ALU = mybir.AluOpType
+ACT = mybir.ActivationFunctionType
+AXIS = mybir.AxisListType
+
+P = 128
+PACK = 4
+D, C, I, Q, E = 512, 1024, 512, 128, 512
+HALF = E // 2
+FLOPS = 2 * Q * I * D + 2 * Q * E * I
+
+
+def tile_attend_pqkeys_kernel(tc, book_words, book_scales, query, size, vals, offs, out):
+    nc = tc.nc
+    with ExitStack() as ctx:
+        sb = ctx.enter_context(tc.tile_pool(name="sb", bufs=1))
+        ps = ctx.enter_context(tc.psum_pool(name="ps", bufs=1))
+
+        scale_win = sb.tile([P, C], U8, name="scale_win", align_bytes=64)
+        rows = book_scales[0].bitcast(I32).rearrange("(h v) c -> h v c", v=2)
+        for v in range(2):
+            (nc.sync, nc.scalar)[v].dma_start(
+                out=scale_win[:].bitcast(I32)[v:P:2, :],
+                in_=rows[:, v, :].unsqueeze(1).to_broadcast([8, 8, C // 4]),
+            )
+        offsets = sb.tile([P, I // 16], U16, name="offsets")
+        nc.sync.dma_start(offsets[:], offs)
+        word_win = sb.tile([P, C], I32, name="word_win", align_bytes=64)
+        nc.sync.dma_start(out=word_win[:], in_=book_words[0].rearrange("p c r -> p (c r)").bitcast(I32))
+        q_raw = sb.tile([P, PACK, Q], F32, name="q_raw")
+        nc.sync.dma_start(out=q_raw[:], in_=query.rearrange("(p j) q -> p j q", j=PACK))
+        v_raw = [sb.tile([P, PACK, HALF], F32, name="v_raw%d" % h) for h in range(2)]
+        v_rows = vals.rearrange("(p j) e -> p j e", j=PACK)
+        for h in range(2):
+            nc.sync.dma_start(out=v_raw[h][:], in_=v_rows[:, :, h * HALF : (h + 1) * HALF])
+        size_col = sb.tile([P, PACK], F32, name="size_col")
+        nc.scalar.dma_start(out=size_col[:], in_=size.rearrange("o (p j) -> (o p) j", j=PACK))
+
+        ident = sb.tile([P, P], F32, name="ident")
+        make_identity(nc, ident[:])
+        warm = sb.tile([P, 2], F32, name="warm")
+        nc.vector.memset(warm[:], 0.0)
+        nc.scalar.activation(warm[:, 1:2], warm[:, 0:1], ACT.Exp)
+
+        key_plane = sb.tile([P, I], U8, name="key_plane", align_bytes=64)
+        nc.vector.memset(key_plane[:].bitcast(I32), 0)
+        got_scales = sb.tile([P, I], U8, name="got_scales", align_bytes=64)
+        nc.vector.tensor_copy(got_scales[:], scale_win[:].indirect(offsets[:]))
+        for v in range(2):
+            nc.scalar.dma_start(
+                out=key_plane[:].bitcast(I32)[2 + v : P : 32, :],
+                in_=got_scales[:].bitcast(I32)[16 + v : P : 32, :],
+            )
+        key_words = sb.tile([P, I], U32, name="key_words", align_bytes=64)
+        nc.vector.tensor_copy(key_words[:], word_win[:].bitcast(U32).indirect(offsets[:]))
+        for x in range(4):
+            nc.vector.tensor_copy(
+                key_plane[:].bitcast(I32)[32 * x : 32 * x + 2, :],
+                got_scales[:].bitcast(I32)[32 * x : 32 * x + 2, :],
+            )
+
+        q_bf = sb.tile([P, Q, PACK], BF16, name="q_bf", align_bytes=64)
+        nc.scalar.copy(q_bf[:], q_raw[:].rearrange("p j q -> p q j"))
+        q_words = sb.tile([P, Q], U32, name="q_words", align_bytes=64)
+        q_plane = sb.tile([P, Q], U8, name="q_plane", align_bytes=64)
+        nc.vector.quantize_mx(q_words[:].bitcast(FP8X4), q_plane[:], q_bf[:].rearrange("p q j -> p (q j)"))
+
+        size_ps = ps.tile([P, PACK, P], F32, name="size_ps")
+        for t in range(PACK):
+            nc.tensor.transpose(size_ps[:, t, :], size_col[:, t : t + 1].to_broadcast([P, P]), ident[:])
+
+        v_bf = [sb.tile([P, HALF, PACK], BF16, name="v_bf%d" % h, align_bytes=64) for h in range(2)]
+        v_words = [sb.tile([P, HALF], U32, name="v_words%d" % h, align_bytes=64) for h in range(2)]
+        v_plane = [sb.tile([P, HALF], U8, name="v_plane%d" % h, align_bytes=64) for h in range(2)]
+
+        def weave(engine_copy, h, a, b):
+            engine_copy(
+                v_bf[h][:, a:b, :].rearrange("p (c i) t -> p c t i", i=4),
+                v_raw[h][:, :, a:b].rearrange("p t (c i) -> p c t i", i=4),
+            )
+
+        def quantise_values(h):
+            nc.vector.quantize_mx(
+                v_words[h][:].bitcast(FP8X4), v_plane[h][:], v_bf[h][:].rearrange("p e j -> p (e j)")
+            )
+
+        weave(nc.scalar.copy, 0, 0, HALF)
+
+        scores = ps.tile([P, I], F32, name="scores")
+        nc.tensor.matmul_mx(
+            scores[:], lhsT=q_words[:].bitcast(FP8X4), lhsT_scale=q_plane[:],
+            rhs=key_words[:].bitcast(FP8X4), rhs_scale=key_plane[:], start=True, stop=True,
+        )
+        neg_max = sb.tile([P, 1], F32, name="neg_max")
+        nc.vector.tensor_reduce(neg_max[:], scores[:], AXIS.X, ALU.max, negate=True)
+        probs = sb.tile([P, 2, P, 2], F32, name="probs")
+        row_sum = sb.tile([P, 1], F32, name="row_sum")
+        nc.scalar.activation(
+            probs[:], scores[:].rearrange("q (s u e) -> q u s e", u=2, e=2), ACT.Exp,
+            bias=neg_max[:], accum_out=row_sum[:],
+        )
+        quantise_values(0)
+        weave(nc.vector.tensor_copy, 1, HALF // 2, HALF)
+        weave(nc.scalar.copy, 1, 0, HALF // 2)
+        inv_sum = sb.tile([P, 1], F32, name="inv_sum")
+        nc.vector.reciprocal(inv_sum[:], row_sum[:])
+
+        w_bf = [sb.tile([P, P, 2], BF16, name="w_bf%d" % u) for u in range(2)]
+        turned = ps.tile([P, 2, Q], F32, name="turned")
+        for u in range(2):
+            nc.vector.scalar_tensor_tensor(
+                w_bf[u][:], probs[:, u, :, :], inv_sum[:],
+                size_ps[:, 2 * u : 2 * u + 2, :].rearrange("q e s -> q s e"), ALU.mult, ALU.mult,
+            )
+            nc.tensor.transpose(
+                turned[:, u, :], w_bf[u][:].rearrange("q s e -> q (s e)").bitcast(F32), ident[:]
+            )
+        quantise_values(1)
+        wt_bf = sb.tile([P, Q * PACK], BF16, name="wt_bf", align_bytes=64)
+        nc.vector.tensor_copy(
+            wt_bf[:].bitcast(F32).rearrange("s (q u) -> s q u", u=2), turned[:].rearrange("s u q -> s q u")
+        )
+        w_words = sb.tile([P, Q], U32, name="w_words", align_bytes=64)
+        w_plane = sb.tile([P, Q], U8, name="w_plane", align_bytes=64)
+        nc.vector.quantize_mx(w_words[:].bitcast(FP8X4), w_plane[:], wt_bf[:])
+
+        copies = (nc.scalar.copy, nc.vector.tensor_copy)
+        queues = (nc.scalar, nc.sync)
+        for h in range(2):
+            acc = ps.tile([P, HALF], F32, name="acc%d" % h)
+            nc.tensor.matmul_mx(
+                acc[:], lhsT=w_words[:].bitcast(FP8X4), lhsT_scale=w_plane[:],
+                rhs=v_words[h][:].bitcast(FP8X4), rhs_scale=v_plane[h][:], start=True, stop=True,
+            )
+            res = sb.tile([P, HALF], F32, name="res%d" % h)
+            copies[h](res[:], acc[:])
+            queues[h].dma_start(out=out[:, h * HALF : (h + 1) * HALF], in_=res[:])

@@ -27,23 +27,20 @@ def tile_attend_pqkeys_kernel(tc, book_words, book_scales, query, size, vals, of
         sb = ctx.enter_context(tc.tile_pool(name="sb", bufs=1))
         ps = ctx.enter_context(tc.psum_pool(name="ps", bufs=1))
 
-        scale_win = sb.tile([P, C], U8, name="scale_win", align_bytes=64)
-        rows = book_scales[0].bitcast(I32).rearrange("(h v) c -> h v c", v=2)
-        for v in range(2):
-            (nc.sync, nc.scalar)[v].dma_start(
-                out=scale_win[:].bitcast(I32)[v:P:2, :],
-                in_=rows[:, v, :].unsqueeze(1).to_broadcast([8, 8, C // 4]),
-            )
+        scale_win = sb.tile([P, C], U8, name="scale_win", tag="scales_then_values", align_bytes=64)
+        nc.sync.dma_start(
+            out=scale_win[:].bitcast(I32),
+            in_=book_scales[0].bitcast(I32).unsqueeze(1).to_broadcast([16, 8, C // 4]),
+        )
         offsets = sb.tile([P, I // 16], U16, name="offsets")
         nc.sync.dma_start(offsets[:], offs)
         word_win = sb.tile([P, C], I32, name="word_win", align_bytes=64)
         nc.sync.dma_start(out=word_win[:], in_=book_words[0].rearrange("p c r -> p (c r)").bitcast(I32))
         q_raw = sb.tile([P, PACK, Q], F32, name="q_raw")
         nc.sync.dma_start(out=q_raw[:], in_=query.rearrange("(p j) q -> p j q", j=PACK))
-        v_raw = [sb.tile([P, PACK, HALF], F32, name="v_raw%d" % h) for h in range(2)]
         v_rows = vals.rearrange("(p j) e -> p j e", j=PACK)
-        for h in range(2):
-            nc.sync.dma_start(out=v_raw[h][:], in_=v_rows[:, :, h * HALF : (h + 1) * HALF])
+        v_raw = [sb.tile([P, PACK, HALF], F32, name="v_raw0")]
+        nc.sync.dma_start(out=v_raw[0][:], in_=v_rows[:, :, 0:HALF])
         size_col = sb.tile([P, PACK], F32, name="size_col")
         nc.scalar.dma_start(out=size_col[:], in_=size.rearrange("o (p j) -> (o p) j", j=PACK))
 
@@ -57,22 +54,19 @@ def tile_attend_pqkeys_kernel(tc, book_words, book_scales, query, size, vals, of
         nc.vector.memset(key_plane[:].bitcast(I32), 0)
         got_scales = sb.tile([P, I], U8, name="got_scales", align_bytes=64)
         nc.vector.tensor_copy(got_scales[:], scale_win[:].indirect(offsets[:]))
-        for v in range(2):
-            nc.scalar.dma_start(
-                out=key_plane[:].bitcast(I32)[2 + v : P : 32, :],
-                in_=got_scales[:].bitcast(I32)[16 + v : P : 32, :],
+        for j in range(4):
+            (nc.sync, nc.scalar)[j % 2].dma_start(
+                out=key_plane[:].bitcast(I32)[j:P:32, :],
+                in_=got_scales[:].bitcast(I32)[8 * j : P : 32, :],
             )
-        key_words = sb.tile([P, I], U32, name="key_words", align_bytes=64)
+        v_raw.append(sb.tile([P, PACK, HALF], F32, name="v_raw1", tag="scales_then_values", align_bytes=64))
+        nc.sync.dma_start(out=v_raw[1][:], in_=v_rows[:, :, HALF:E])
+        key_words = sb.tile([P, I], U32, name="key_words", tag="keys_then_values", align_bytes=64)
         nc.vector.tensor_copy(key_words[:], word_win[:].bitcast(U32).indirect(offsets[:]))
-        for x in range(4):
-            nc.vector.tensor_copy(
-                key_plane[:].bitcast(I32)[32 * x : 32 * x + 2, :],
-                got_scales[:].bitcast(I32)[32 * x : 32 * x + 2, :],
-            )
 
         q_bf = sb.tile([P, Q, PACK], BF16, name="q_bf", align_bytes=64)
         nc.scalar.copy(q_bf[:], q_raw[:].rearrange("p j q -> p q j"))
-        q_words = sb.tile([P, Q], U32, name="q_words", align_bytes=64)
+        q_words = sb.tile([P, Q], U32, name="q_words", tag="queries_then_values", align_bytes=64)
         q_plane = sb.tile([P, Q], U8, name="q_plane", align_bytes=64)
         nc.vector.quantize_mx(q_words[:].bitcast(FP8X4), q_plane[:], q_bf[:].rearrange("p q j -> p (q j)"))
 
@@ -80,29 +74,24 @@ def tile_attend_pqkeys_kernel(tc, book_words, book_scales, query, size, vals, of
         for t in range(PACK):
             nc.tensor.transpose(size_ps[:, t, :], size_col[:, t : t + 1].to_broadcast([P, P]), ident[:])
 
-        v_bf = [sb.tile([P, HALF, PACK], BF16, name="v_bf%d" % h, align_bytes=64) for h in range(2)]
-        v_words = [sb.tile([P, HALF], U32, name="v_words%d" % h, align_bytes=64) for h in range(2)]
-        v_plane = [sb.tile([P, HALF], U8, name="v_plane%d" % h, align_bytes=64) for h in range(2)]
-
-        def weave(engine_copy, h, a, b):
+        def weave(engine_copy, dst, h, a, b):
             engine_copy(
-                v_bf[h][:, a:b, :].rearrange("p (c i) t -> p c t i", i=4),
+                dst[:].rearrange("p (c i) t -> p c t i", i=4),
                 v_raw[h][:, :, a:b].rearrange("p t (c i) -> p c t i", i=4),
             )
 
-        def quantise_values(h):
-            nc.vector.quantize_mx(
-                v_words[h][:].bitcast(FP8X4), v_plane[h][:], v_bf[h][:].rearrange("p e j -> p (e j)")
-            )
+        def quantise_values(words, plane, src):
+            nc.vector.quantize_mx(words.bitcast(FP8X4), plane, src[:].rearrange("p e j -> p (e j)"))
 
-        weave(nc.scalar.copy, 0, 0, HALF)
+        v_bf0 = sb.tile([P, HALF, PACK], BF16, name="v_bf0", align_bytes=64)
+        weave(nc.scalar.copy, v_bf0, 0, 0, HALF)
 
         scores = ps.tile([P, I], F32, name="scores")
         nc.tensor.matmul_mx(
             scores[:], lhsT=q_words[:].bitcast(FP8X4), lhsT_scale=q_plane[:],
             rhs=key_words[:].bitcast(FP8X4), rhs_scale=key_plane[:], start=True, stop=True,
         )
-        neg_max = sb.tile([P, 1], F32, name="neg_max")
+        neg_max = sb.tile([P, 1], F32, name="neg_max", tag="max_then_values", align_bytes=64)
         nc.vector.tensor_reduce(neg_max[:], scores[:], AXIS.X, ALU.max, negate=True)
         probs = sb.tile([P, 2, P, 2], F32, name="probs")
         row_sum = sb.tile([P, 1], F32, name="row_sum")
@@ -110,9 +99,17 @@ def tile_attend_pqkeys_kernel(tc, book_words, book_scales, query, size, vals, of
             probs[:], scores[:].rearrange("q (s u e) -> q u s e", u=2, e=2), ACT.Exp,
             bias=neg_max[:], accum_out=row_sum[:],
         )
-        quantise_values(0)
-        weave(nc.vector.tensor_copy, 1, HALF // 2, HALF)
-        weave(nc.scalar.copy, 1, 0, HALF // 2)
+        v_words = [
+            sb.tile([P, HALF], U32, name="v_words0", tag="queries_then_values", align_bytes=64),
+            sb.tile([P, HALF], U32, name="v_words1", align_bytes=64),
+        ]
+        v_plane = [sb.tile([P, HALF], U8, name="v_plane%d" % h, align_bytes=64) for h in range(2)]
+        quarter = HALF // 2
+        v_bf2 = sb.tile([P, quarter, PACK], BF16, name="v_bf2", tag="keys_then_values", align_bytes=64)
+        v_bf3 = sb.tile([P, quarter, PACK], BF16, name="v_bf3", tag="max_then_values", align_bytes=64)
+        weave(nc.vector.tensor_copy, v_bf2, 1, 0, quarter)
+        quantise_values(v_words[0][:], v_plane[0][:], v_bf0)
+        weave(nc.scalar.copy, v_bf3, 1, quarter, HALF)
         inv_sum = sb.tile([P, 1], F32, name="inv_sum")
         nc.vector.reciprocal(inv_sum[:], row_sum[:])
 
@@ -126,23 +123,27 @@ def tile_attend_pqkeys_kernel(tc, book_words, book_scales, query, size, vals, of
             nc.tensor.transpose(
                 turned[:, u, :], w_bf[u][:].rearrange("q s e -> q (s e)").bitcast(F32), ident[:]
             )
-        quantise_values(1)
+        quantise_values(v_words[1][:, 0:quarter], v_plane[1][:, 0:quarter], v_bf2)
+        quantise_values(v_words[1][:, quarter:HALF], v_plane[1][:, quarter:HALF], v_bf3)
         wt_bf = sb.tile([P, Q * PACK], BF16, name="wt_bf", align_bytes=64)
-        nc.vector.tensor_copy(
+        nc.scalar.copy(
             wt_bf[:].bitcast(F32).rearrange("s (q u) -> s q u", u=2), turned[:].rearrange("s u q -> s q u")
         )
         w_words = sb.tile([P, Q], U32, name="w_words", align_bytes=64)
         w_plane = sb.tile([P, Q], U8, name="w_plane", align_bytes=64)
         nc.vector.quantize_mx(w_words[:].bitcast(FP8X4), w_plane[:], wt_bf[:])
 
-        copies = (nc.scalar.copy, nc.vector.tensor_copy)
-        queues = (nc.scalar, nc.sync)
-        for h in range(2):
-            acc = ps.tile([P, HALF], F32, name="acc%d" % h)
+        pieces = (
+            (0, 0, HALF, nc.scalar.copy, nc.scalar),
+            (1, 0, quarter, nc.vector.tensor_copy, nc.sync),
+            (1, quarter, HALF, nc.vector.tensor_copy, nc.sync),
+        )
+        for n, (h, a, b, copy, queue) in enumerate(pieces):
+            acc = ps.tile([P, b - a], F32, name="acc%d" % n)
             nc.tensor.matmul_mx(
                 acc[:], lhsT=w_words[:].bitcast(FP8X4), lhsT_scale=w_plane[:],
-                rhs=v_words[h][:].bitcast(FP8X4), rhs_scale=v_plane[h][:], start=True, stop=True,
+                rhs=v_words[h][:, a:b].bitcast(FP8X4), rhs_scale=v_plane[h][:, a:b], start=True, stop=True,
             )
-            res = sb.tile([P, HALF], F32, name="res%d" % h)
-            copies[h](res[:], acc[:])
-            queues[h].dma_start(out=out[:, h * HALF : (h + 1) * HALF], in_=res[:])
+            res = sb.tile([P, b - a], F32, name="res%d" % n)
+            copy(res[:], acc[:])
+            queue.dma_start(out=out[:, h * HALF + a : h * HALF + b], in_=res[:])

@@ -16,8 +16,13 @@ AXIS = mybir.AxisListType
 
 P = 128
 PACK = 4
+BLOCK_ROWS = 8
+QUADRANT = 32
+GROUP = 16
 D, C, I, Q, E = 512, 1024, 512, 128, 512
 HALF = E // 2
+QUARTER = E // 4
+MX_ALIGN = 64
 FLOPS = 2 * Q * I * D + 2 * Q * E * I
 
 
@@ -27,123 +32,121 @@ def tile_attend_pqkeys_kernel(tc, book_words, book_scales, query, size, vals, of
         sb = ctx.enter_context(tc.tile_pool(name="sb", bufs=1))
         ps = ctx.enter_context(tc.psum_pool(name="ps", bufs=1))
 
-        scale_win = sb.tile([P, C], U8, name="scale_win", tag="scales_then_values", align_bytes=64)
+        scale_win = sb.tile([P, C], U8, name="scale_win", tag="scales_then_values", align_bytes=MX_ALIGN)
         nc.sync.dma_start(
             out=scale_win[:].bitcast(I32),
-            in_=book_scales[0].bitcast(I32).unsqueeze(1).to_broadcast([16, 8, C // 4]),
+            in_=book_scales[0].bitcast(I32).unsqueeze(1).to_broadcast([P // BLOCK_ROWS, BLOCK_ROWS, C // 4]),
         )
-        offsets = sb.tile([P, I // 16], U16, name="offsets")
+        offsets = sb.tile([P, I // GROUP], U16, name="offsets")
         nc.sync.dma_start(offsets[:], offs)
-        word_win = sb.tile([P, C], I32, name="word_win", align_bytes=64)
+        word_win = sb.tile([P, C], I32, name="word_win", align_bytes=MX_ALIGN)
         nc.sync.dma_start(out=word_win[:], in_=book_words[0].rearrange("p c r -> p (c r)").bitcast(I32))
         q_raw = sb.tile([P, PACK, Q], F32, name="q_raw")
-        nc.sync.dma_start(out=q_raw[:], in_=query.rearrange("(p j) q -> p j q", j=PACK))
-        v_rows = vals.rearrange("(p j) e -> p j e", j=PACK)
-        v_raw = [sb.tile([P, PACK, HALF], F32, name="v_raw0")]
-        nc.sync.dma_start(out=v_raw[0][:], in_=v_rows[:, :, 0:HALF])
+        nc.sync.dma_start(out=q_raw[:], in_=query.rearrange("(p t) q -> p t q", t=PACK))
+        v_rows = vals.rearrange("(p t) e -> p t e", t=PACK)
+        v_raw_first = sb.tile([P, PACK, HALF], F32, name="v_raw_first")
+        nc.sync.dma_start(out=v_raw_first[:], in_=v_rows[:, :, 0:HALF])
         size_col = sb.tile([P, PACK], F32, name="size_col")
-        nc.scalar.dma_start(out=size_col[:], in_=size.rearrange("o (p j) -> (o p) j", j=PACK))
+        nc.scalar.dma_start(out=size_col[:], in_=size.rearrange("o (p t) -> (o p) t", t=PACK))
 
         ident = sb.tile([P, P], F32, name="ident")
-        make_identity(nc, ident[:])
-        warm = sb.tile([P, 2], F32, name="warm")
-        nc.vector.memset(warm[:], 0.0)
-        nc.scalar.activation(warm[:, 1:2], warm[:, 0:1], ACT.Exp)
+        zero = sb.tile([P, 1], F32, name="zero")
+        nc.vector.memset(zero[:], 0.0)
+        nc.scalar.copy(ident[:], zero[:].to_broadcast([P, P]))
+        make_identity(nc, ident[:], nomemset=True)
 
-        key_plane = sb.tile([P, I], U8, name="key_plane", align_bytes=64)
+        key_plane = sb.tile([P, I], U8, name="key_plane", align_bytes=MX_ALIGN)
         nc.vector.memset(key_plane[:].bitcast(I32), 0)
-        got_scales = sb.tile([P, I], U8, name="got_scales", align_bytes=64)
+        got_scales = sb.tile([P, I], U8, name="got_scales", align_bytes=MX_ALIGN)
         nc.vector.tensor_copy(got_scales[:], scale_win[:].indirect(offsets[:]))
-        for j in range(4):
+        for j in range(QUADRANT // BLOCK_ROWS):
             (nc.sync, nc.scalar)[j % 2].dma_start(
-                out=key_plane[:].bitcast(I32)[j:P:32, :],
-                in_=got_scales[:].bitcast(I32)[8 * j : P : 32, :],
+                out=key_plane[:].bitcast(I32)[j:P:QUADRANT, :],
+                in_=got_scales[:].bitcast(I32)[BLOCK_ROWS * j : P : QUADRANT, :],
             )
-        v_raw.append(sb.tile([P, PACK, HALF], F32, name="v_raw1", tag="scales_then_values", align_bytes=64))
-        nc.sync.dma_start(out=v_raw[1][:], in_=v_rows[:, :, HALF:E])
-        key_words = sb.tile([P, I], U32, name="key_words", tag="keys_then_values", align_bytes=64)
+        v_raw_second = sb.tile([P, PACK, HALF], F32, name="v_raw_second", tag="scales_then_values", align_bytes=MX_ALIGN)
+        nc.sync.dma_start(out=v_raw_second[:], in_=v_rows[:, :, HALF:E])
+        key_words = sb.tile([P, I], U32, name="key_words", align_bytes=MX_ALIGN)
         nc.vector.tensor_copy(key_words[:], word_win[:].bitcast(U32).indirect(offsets[:]))
 
-        q_bf = sb.tile([P, Q, PACK], BF16, name="q_bf", align_bytes=64)
-        nc.scalar.copy(q_bf[:], q_raw[:].rearrange("p j q -> p q j"))
-        q_words = sb.tile([P, Q], U32, name="q_words", tag="queries_then_values", align_bytes=64)
-        q_plane = sb.tile([P, Q], U8, name="q_plane", align_bytes=64)
-        nc.vector.quantize_mx(q_words[:].bitcast(FP8X4), q_plane[:], q_bf[:].rearrange("p q j -> p (q j)"))
+        q_bf = sb.tile([P, Q, PACK], BF16, name="q_bf", align_bytes=MX_ALIGN)
+        nc.scalar.copy(q_bf[:], q_raw[:].rearrange("p t q -> p q t"))
+        q_words = sb.tile([P, Q], U32, name="q_words", tag="queries_then_values", align_bytes=MX_ALIGN)
+        q_plane = sb.tile([P, Q], U8, name="q_plane", align_bytes=MX_ALIGN)
+        nc.vector.quantize_mx(q_words[:].bitcast(FP8X4), q_plane[:], q_bf[:].rearrange("p q t -> p (q t)"))
 
         size_ps = ps.tile([P, PACK, P], F32, name="size_ps")
         for t in range(PACK):
             nc.tensor.transpose(size_ps[:, t, :], size_col[:, t : t + 1].to_broadcast([P, P]), ident[:])
 
-        def weave(engine_copy, dst, h, a, b):
-            engine_copy(
-                dst[:].rearrange("p (c i) t -> p c t i", i=4),
-                v_raw[h][:, :, a:b].rearrange("p t (c i) -> p c t i", i=4),
-            )
+        def interleave(copy, dst, src):
+            copy(dst.rearrange("p (c n) t -> p c t n", n=4), src.rearrange("p t (c n) -> p c t n", n=4))
 
         def quantise_values(words, plane, src):
-            nc.vector.quantize_mx(words.bitcast(FP8X4), plane, src[:].rearrange("p e j -> p (e j)"))
+            nc.vector.quantize_mx(words.bitcast(FP8X4), plane, src.rearrange("p e t -> p (e t)"))
 
-        v_bf0 = sb.tile([P, HALF, PACK], BF16, name="v_bf0", align_bytes=64)
-        weave(nc.scalar.copy, v_bf0, 0, 0, HALF)
+        v_bf_first = sb.tile([P, HALF, PACK], BF16, name="v_bf_first", align_bytes=MX_ALIGN)
+        interleave(nc.scalar.copy, v_bf_first[:], v_raw_first[:])
 
         scores = ps.tile([P, I], F32, name="scores")
         nc.tensor.matmul_mx(
             scores[:], lhsT=q_words[:].bitcast(FP8X4), lhsT_scale=q_plane[:],
             rhs=key_words[:].bitcast(FP8X4), rhs_scale=key_plane[:], start=True, stop=True,
         )
-        neg_max = sb.tile([P, 1], F32, name="neg_max", tag="max_then_values", align_bytes=64)
+        neg_max = sb.tile([P, 1], F32, name="neg_max", tag="max_then_values", align_bytes=MX_ALIGN)
         nc.vector.tensor_reduce(neg_max[:], scores[:], AXIS.X, ALU.max, negate=True)
-        probs = sb.tile([P, 2, P, 2], F32, name="probs")
+        probs = sb.tile([P, 2, P, 2], F32, name="probs", tag="probs_then_values", align_bytes=MX_ALIGN)
         row_sum = sb.tile([P, 1], F32, name="row_sum")
         nc.scalar.activation(
-            probs[:], scores[:].rearrange("q (s u e) -> q u s e", u=2, e=2), ACT.Exp,
+            probs[:], scores[:].rearrange("q (s u r) -> q u s r", u=2, r=2), ACT.Exp,
             bias=neg_max[:], accum_out=row_sum[:],
         )
-        v_words = [
-            sb.tile([P, HALF], U32, name="v_words0", tag="queries_then_values", align_bytes=64),
-            sb.tile([P, HALF], U32, name="v_words1", align_bytes=64),
-        ]
-        v_plane = [sb.tile([P, HALF], U8, name="v_plane%d" % h, align_bytes=64) for h in range(2)]
-        quarter = HALF // 2
-        v_bf2 = sb.tile([P, quarter, PACK], BF16, name="v_bf2", tag="keys_then_values", align_bytes=64)
-        v_bf3 = sb.tile([P, quarter, PACK], BF16, name="v_bf3", tag="max_then_values", align_bytes=64)
-        weave(nc.vector.tensor_copy, v_bf2, 1, 0, quarter)
-        quantise_values(v_words[0][:], v_plane[0][:], v_bf0)
-        weave(nc.scalar.copy, v_bf3, 1, quarter, HALF)
+
+        v_words_first = sb.tile([P, HALF], U32, name="v_words_first", tag="queries_then_values", align_bytes=MX_ALIGN)
+        v_plane_first = sb.tile([P, HALF], U8, name="v_plane_first", align_bytes=MX_ALIGN)
+        quantise_values(v_words_first[:], v_plane_first[:], v_bf_first[:])
+        v_bf_fourth = sb.tile([P, QUARTER, PACK], BF16, name="v_bf_fourth", tag="max_then_values", align_bytes=MX_ALIGN)
+        interleave(nc.scalar.copy, v_bf_fourth[:], v_raw_second[:, :, QUARTER:HALF])
+
         inv_sum = sb.tile([P, 1], F32, name="inv_sum")
         nc.vector.reciprocal(inv_sum[:], row_sum[:])
-
-        w_bf = [sb.tile([P, P, 2], BF16, name="w_bf%d" % u) for u in range(2)]
         turned = ps.tile([P, 2, Q], F32, name="turned")
         for u in range(2):
+            w_pair = sb.tile([P, P, 2], BF16, name="w_pair%d" % u)
             nc.vector.scalar_tensor_tensor(
-                w_bf[u][:], probs[:, u, :, :], inv_sum[:],
-                size_ps[:, 2 * u : 2 * u + 2, :].rearrange("q e s -> q s e"), ALU.mult, ALU.mult,
+                w_pair[:], probs[:, u, :, :], inv_sum[:],
+                size_ps[:, 2 * u : 2 * u + 2, :].rearrange("q r s -> q s r"), ALU.mult, ALU.mult,
             )
             nc.tensor.transpose(
-                turned[:, u, :], w_bf[u][:].rearrange("q s e -> q (s e)").bitcast(F32), ident[:]
+                turned[:, u, :], w_pair[:].rearrange("q s r -> q (s r)").bitcast(F32), ident[:]
             )
-        quantise_values(v_words[1][:, 0:quarter], v_plane[1][:, 0:quarter], v_bf2)
-        quantise_values(v_words[1][:, quarter:HALF], v_plane[1][:, quarter:HALF], v_bf3)
-        wt_bf = sb.tile([P, Q * PACK], BF16, name="wt_bf", align_bytes=64)
+
+        v_bf_third = sb.tile([P, QUARTER, PACK], BF16, name="v_bf_third", tag="probs_then_values", align_bytes=MX_ALIGN)
+        interleave(nc.vector.tensor_copy, v_bf_third[:], v_raw_second[:, :, 0:QUARTER])
+        v_words_second = sb.tile([P, HALF], U32, name="v_words_second", align_bytes=MX_ALIGN)
+        v_plane_second = sb.tile([P, HALF], U8, name="v_plane_second", align_bytes=MX_ALIGN)
+        quantise_values(v_words_second[:, QUARTER:HALF], v_plane_second[:, QUARTER:HALF], v_bf_fourth[:])
+        quantise_values(v_words_second[:, 0:QUARTER], v_plane_second[:, 0:QUARTER], v_bf_third[:])
+
+        wt_bf = sb.tile([P, Q * PACK], BF16, name="wt_bf", align_bytes=MX_ALIGN)
         nc.scalar.copy(
             wt_bf[:].bitcast(F32).rearrange("s (q u) -> s q u", u=2), turned[:].rearrange("s u q -> s q u")
         )
-        w_words = sb.tile([P, Q], U32, name="w_words", align_bytes=64)
-        w_plane = sb.tile([P, Q], U8, name="w_plane", align_bytes=64)
+        w_words = sb.tile([P, Q], U32, name="w_words", align_bytes=MX_ALIGN)
+        w_plane = sb.tile([P, Q], U8, name="w_plane", align_bytes=MX_ALIGN)
         nc.vector.quantize_mx(w_words[:].bitcast(FP8X4), w_plane[:], wt_bf[:])
 
         pieces = (
-            (0, 0, HALF, nc.scalar.copy, nc.scalar),
-            (1, 0, quarter, nc.vector.tensor_copy, nc.sync),
-            (1, quarter, HALF, nc.vector.tensor_copy, nc.sync),
+            (v_words_first[:], v_plane_first[:], 0, HALF, nc.scalar.copy, nc.scalar),
+            (v_words_second[:, 0:QUARTER], v_plane_second[:, 0:QUARTER], HALF, QUARTER, nc.vector.tensor_copy, nc.sync),
+            (v_words_second[:, QUARTER:HALF], v_plane_second[:, QUARTER:HALF], HALF + QUARTER, QUARTER, nc.vector.tensor_copy, nc.sync),
         )
-        for n, (h, a, b, copy, queue) in enumerate(pieces):
-            acc = ps.tile([P, b - a], F32, name="acc%d" % n)
+        for n, (words, plane, first, width, copy, queue) in enumerate(pieces):
+            acc = ps.tile([P, width], F32, name="acc%d" % n)
             nc.tensor.matmul_mx(
                 acc[:], lhsT=w_words[:].bitcast(FP8X4), lhsT_scale=w_plane[:],
-                rhs=v_words[h][:, a:b].bitcast(FP8X4), rhs_scale=v_plane[h][:, a:b], start=True, stop=True,
+                rhs=words.bitcast(FP8X4), rhs_scale=plane, start=True, stop=True,
             )
-            res = sb.tile([P, b - a], F32, name="res%d" % n)
+            res = sb.tile([P, width], F32, name="res%d" % n)
             copy(res[:], acc[:])
-            queue.dma_start(out=out[:, h * HALF + a : h * HALF + b], in_=res[:])
+            queue.dma_start(out=out[:, first : first + width], in_=res[:])

@@ -32,14 +32,14 @@ def tile_attend_pqkeys_kernel(tc, book_words, book_scales, query, size, vals, of
         sb = ctx.enter_context(tc.tile_pool(name="sb", bufs=1))
         ps = ctx.enter_context(tc.psum_pool(name="ps", bufs=1))
 
-        scale_win = sb.tile([P, C], U8, name="scale_win", tag="scales_then_values", align_bytes=MX_ALIGN)
+        scale_win = sb.tile([P, C], U8, name="scale_win", align_bytes=MX_ALIGN)
         nc.sync.dma_start(
             out=scale_win[:].bitcast(I32),
             in_=book_scales[0].bitcast(I32).unsqueeze(1).to_broadcast([P // BLOCK_ROWS, BLOCK_ROWS, C // 4]),
         )
         offsets = sb.tile([P, I // GROUP], U16, name="offsets")
         nc.sync.dma_start(offsets[:], offs)
-        word_win = sb.tile([P, C], I32, name="word_win", align_bytes=MX_ALIGN)
+        word_win = sb.tile([P, C], I32, name="word_win", tag="words_then_values", align_bytes=MX_ALIGN)
         nc.sync.dma_start(out=word_win[:], in_=book_words[0].rearrange("p c r -> p (c r)").bitcast(I32))
         q_raw = sb.tile([P, PACK, Q], F32, name="q_raw")
         nc.sync.dma_start(out=q_raw[:], in_=query.rearrange("(p t) q -> p t q", t=PACK))
@@ -64,10 +64,10 @@ def tile_attend_pqkeys_kernel(tc, book_words, book_scales, query, size, vals, of
                 out=key_plane[:].bitcast(I32)[j:P:QUADRANT, :],
                 in_=got_scales[:].bitcast(I32)[BLOCK_ROWS * j : P : QUADRANT, :],
             )
-        v_raw_second = sb.tile([P, PACK, HALF], F32, name="v_raw_second", tag="scales_then_values", align_bytes=MX_ALIGN)
-        nc.sync.dma_start(out=v_raw_second[:], in_=v_rows[:, :, HALF:E])
         key_words = sb.tile([P, I], U32, name="key_words", align_bytes=MX_ALIGN)
         nc.vector.tensor_copy(key_words[:], word_win[:].bitcast(U32).indirect(offsets[:]))
+        v_raw_second = sb.tile([P, PACK, HALF], F32, name="v_raw_second", tag="words_then_values", align_bytes=MX_ALIGN)
+        nc.sync.dma_start(out=v_raw_second[:], in_=v_rows[:, :, HALF:E])
 
         q_bf = sb.tile([P, Q, PACK], BF16, name="q_bf", align_bytes=MX_ALIGN)
         nc.scalar.copy(q_bf[:], q_raw[:].rearrange("p t q -> p q t"))

@@ -111,14 +111,17 @@ def tile_attend_pqkeys_kernel(tc, book_words, book_scales, query, size, vals, of
         inv_sum = sb.tile([P, 1], F32, name="inv_sum")
         nc.vector.reciprocal(inv_sum[:], row_sum[:])
         turned = ps.tile([P, 2, Q], F32, name="turned")
+        w_pairs = [sb.tile([P, P, 2], BF16, name="w_pair%d" % u) for u in range(2)]
+        size_pairs = [size_ps[:, 2 * u : 2 * u + 2, :].rearrange("q r s -> q s r") for u in range(2)]
+        sized = sb.tile([P, P, 2], F32, name="sized")
+        nc.vector.tensor_tensor(sized[:], probs[:, 1, :, :], size_pairs[1], ALU.mult)
+        nc.vector.scalar_tensor_tensor(
+            w_pairs[0][:], probs[:, 0, :, :], inv_sum[:], size_pairs[0], ALU.mult, ALU.mult
+        )
+        nc.vector.tensor_scalar(w_pairs[1][:], sized[:], inv_sum[:], None, ALU.mult)
         for u in range(2):
-            w_pair = sb.tile([P, P, 2], BF16, name="w_pair%d" % u)
-            nc.vector.scalar_tensor_tensor(
-                w_pair[:], probs[:, u, :, :], inv_sum[:],
-                size_ps[:, 2 * u : 2 * u + 2, :].rearrange("q r s -> q s r"), ALU.mult, ALU.mult,
-            )
             nc.tensor.transpose(
-                turned[:, u, :], w_pair[:].rearrange("q s r -> q (s r)").bitcast(F32), ident[:]
+                turned[:, u, :], w_pairs[u][:].rearrange("q s r -> q (s r)").bitcast(F32), ident[:]
             )
 
         v_bf_third = sb.tile([P, QUARTER, PACK], BF16, name="v_bf_third", tag="probs_then_values", align_bytes=MX_ALIGN)
@@ -128,17 +131,20 @@ def tile_attend_pqkeys_kernel(tc, book_words, book_scales, query, size, vals, of
         quantise_values(v_words_second[:, QUARTER:HALF], v_plane_second[:, QUARTER:HALF], v_bf_fourth[:])
         quantise_values(v_words_second[:, 0:QUARTER], v_plane_second[:, 0:QUARTER], v_bf_third[:])
 
-        wt_bf = sb.tile([P, Q * PACK], BF16, name="wt_bf", align_bytes=MX_ALIGN)
-        nc.scalar.copy(
-            wt_bf[:].bitcast(F32).rearrange("s (q u) -> s q u", u=2), turned[:].rearrange("s u q -> s q u")
-        )
         w_words = sb.tile([P, Q], U32, name="w_words", align_bytes=MX_ALIGN)
         w_plane = sb.tile([P, Q], U8, name="w_plane", align_bytes=MX_ALIGN)
-        nc.vector.quantize_mx(w_words[:].bitcast(FP8X4), w_plane[:], wt_bf[:])
+        for rows in (slice(0, Q // 2), slice(Q // 2, Q)):
+            wt_bf = sb.tile([P, Q // 2 * PACK], BF16, name="wt_bf%d" % rows.start, align_bytes=MX_ALIGN)
+            nc.scalar.copy(
+                wt_bf[:].bitcast(F32).rearrange("s (q u) -> s q u", u=2),
+                turned[:, :, rows].rearrange("s u q -> s q u"),
+            )
+            nc.vector.quantize_mx(w_words[:, rows].bitcast(FP8X4), w_plane[:, rows], wt_bf[:])
 
         pieces = (
-            (v_words_first[:], v_plane_first[:], 0, HALF, nc.scalar.copy, nc.scalar),
-            (v_words_second[:, 0:QUARTER], v_plane_second[:, 0:QUARTER], HALF, QUARTER, nc.vector.tensor_copy, nc.sync),
+            (v_words_first[:, 0:QUARTER], v_plane_first[:, 0:QUARTER], 0, QUARTER, nc.scalar.copy, nc.sync),
+            (v_words_first[:, QUARTER:HALF], v_plane_first[:, QUARTER:HALF], QUARTER, QUARTER, nc.vector.tensor_copy, nc.sync),
+            (v_words_second[:, 0:QUARTER], v_plane_second[:, 0:QUARTER], HALF, QUARTER, nc.scalar.copy, nc.scalar),
             (v_words_second[:, QUARTER:HALF], v_plane_second[:, QUARTER:HALF], HALF + QUARTER, QUARTER, nc.vector.tensor_copy, nc.sync),
         )
         for n, (words, plane, first, width, copy, queue) in enumerate(pieces):

@@ -32,7 +32,7 @@ def tile_attend_pqkeys_kernel(tc, book_words, book_scales, query, size, vals, of
         sb = ctx.enter_context(tc.tile_pool(name="sb", bufs=1))
         ps = ctx.enter_context(tc.psum_pool(name="ps", bufs=1))
 
-        scale_win = sb.tile([P, C], U8, name="scale_win", align_bytes=MX_ALIGN)
+        scale_win = sb.tile([P, C], U8, name="scale_win", tag="scales_then_values", align_bytes=MX_ALIGN)
         nc.sync.dma_start(
             out=scale_win[:].bitcast(I32),
             in_=book_scales[0].bitcast(I32).unsqueeze(1).to_broadcast([P // BLOCK_ROWS, BLOCK_ROWS, C // 4]),
@@ -44,8 +44,8 @@ def tile_attend_pqkeys_kernel(tc, book_words, book_scales, query, size, vals, of
         q_raw = sb.tile([P, PACK, Q], F32, name="q_raw")
         nc.sync.dma_start(out=q_raw[:], in_=query.rearrange("(p t) q -> p t q", t=PACK))
         v_rows = vals.rearrange("(p t) e -> p t e", t=PACK)
-        v_raw_first = sb.tile([P, PACK, HALF], F32, name="v_raw_first")
-        nc.sync.dma_start(out=v_raw_first[:], in_=v_rows[:, :, 0:HALF])
+        v_raw_first = sb.tile([P, PACK, QUARTER], F32, name="v_raw_first")
+        nc.sync.dma_start(out=v_raw_first[:], in_=v_rows[:, :, 0:QUARTER])
         size_col = sb.tile([P, PACK], F32, name="size_col")
         nc.scalar.dma_start(out=size_col[:], in_=size.rearrange("o (p t) -> (o p) t", t=PACK))
 
@@ -64,6 +64,8 @@ def tile_attend_pqkeys_kernel(tc, book_words, book_scales, query, size, vals, of
                 out=key_plane[:].bitcast(I32)[j:P:QUADRANT, :],
                 in_=got_scales[:].bitcast(I32)[BLOCK_ROWS * j : P : QUADRANT, :],
             )
+        v_raw_next = sb.tile([P, PACK, QUARTER], F32, name="v_raw_next", tag="scales_then_values", align_bytes=MX_ALIGN)
+        nc.sync.dma_start(out=v_raw_next[:], in_=v_rows[:, :, QUARTER:HALF])
         key_words = sb.tile([P, I], U32, name="key_words", align_bytes=MX_ALIGN)
         nc.vector.tensor_copy(key_words[:], word_win[:].bitcast(U32).indirect(offsets[:]))
         v_raw_second = sb.tile([P, PACK, HALF], F32, name="v_raw_second", tag="words_then_values", align_bytes=MX_ALIGN)
@@ -85,7 +87,7 @@ def tile_attend_pqkeys_kernel(tc, book_words, book_scales, query, size, vals, of
         def quantise_values(words, plane, src):
             nc.vector.quantize_mx(words.bitcast(FP8X4), plane, src.rearrange("p e t -> p (e t)"))
 
-        v_bf_first = sb.tile([P, HALF, PACK], BF16, name="v_bf_first", align_bytes=MX_ALIGN)
+        v_bf_first = sb.tile([P, QUARTER, PACK], BF16, name="v_bf_first", align_bytes=MX_ALIGN)
         interleave(nc.scalar.copy, v_bf_first[:], v_raw_first[:])
 
         scores = ps.tile([P, I], F32, name="scores")
@@ -102,18 +104,19 @@ def tile_attend_pqkeys_kernel(tc, book_words, book_scales, query, size, vals, of
             bias=neg_max[:], accum_out=row_sum[:],
         )
 
-        v_words_first = sb.tile([P, HALF], U32, name="v_words_first", tag="queries_then_values", align_bytes=MX_ALIGN)
+        v_words_first = sb.tile([P, QUARTER], U32, name="v_words_first", tag="queries_then_values", align_bytes=MX_ALIGN)
         v_plane_first = sb.tile([P, HALF], U8, name="v_plane_first", align_bytes=MX_ALIGN)
-        quantise_values(v_words_first[:], v_plane_first[:], v_bf_first[:])
-        v_bf_fourth = sb.tile([P, QUARTER, PACK], BF16, name="v_bf_fourth", tag="max_then_values", align_bytes=MX_ALIGN)
-        interleave(nc.scalar.copy, v_bf_fourth[:], v_raw_second[:, :, QUARTER:HALF])
+        quantise_values(v_words_first[:, 0:QUARTER], v_plane_first[:, 0:QUARTER], v_bf_first[:])
+        v_bf_late = sb.tile([P, 2, QUARTER, PACK], BF16, name="v_bf_late", tag="max_then_values", align_bytes=MX_ALIGN)
+        interleave(nc.scalar.copy, v_bf_late[:, 0], v_raw_next[:])
+        interleave(nc.scalar.copy, v_bf_late[:, 1], v_raw_second[:, :, QUARTER:HALF])
 
         inv_sum = sb.tile([P, 1], F32, name="inv_sum")
         nc.vector.reciprocal(inv_sum[:], row_sum[:])
         turned = ps.tile([P, 2, Q], F32, name="turned")
         w_pairs = [sb.tile([P, P, 2], BF16, name="w_pair%d" % u) for u in range(2)]
         size_pairs = [size_ps[:, 2 * u : 2 * u + 2, :].rearrange("q r s -> q s r") for u in range(2)]
-        sized = sb.tile([P, P, 2], F32, name="sized")
+        sized = sb.tile([P, P, 2], F32, name="sized", tag="sized_then_values", align_bytes=MX_ALIGN)
         nc.vector.tensor_tensor(sized[:], probs[:, 1, :, :], size_pairs[1], ALU.mult)
         nc.vector.scalar_tensor_tensor(
             w_pairs[0][:], probs[:, 0, :, :], inv_sum[:], size_pairs[0], ALU.mult, ALU.mult
@@ -128,8 +131,10 @@ def tile_attend_pqkeys_kernel(tc, book_words, book_scales, query, size, vals, of
         interleave(nc.vector.tensor_copy, v_bf_third[:], v_raw_second[:, :, 0:QUARTER])
         v_words_second = sb.tile([P, HALF], U32, name="v_words_second", align_bytes=MX_ALIGN)
         v_plane_second = sb.tile([P, HALF], U8, name="v_plane_second", align_bytes=MX_ALIGN)
-        quantise_values(v_words_second[:, QUARTER:HALF], v_plane_second[:, QUARTER:HALF], v_bf_fourth[:])
+        v_words_next = sb.tile([P, QUARTER], U32, name="v_words_next", tag="sized_then_values", align_bytes=MX_ALIGN)
+        quantise_values(v_words_next[:], v_plane_first[:, QUARTER:HALF], v_bf_late[:, 0])
         quantise_values(v_words_second[:, 0:QUARTER], v_plane_second[:, 0:QUARTER], v_bf_third[:])
+        quantise_values(v_words_second[:, QUARTER:HALF], v_plane_second[:, QUARTER:HALF], v_bf_late[:, 1])
 
         w_words = sb.tile([P, Q], U32, name="w_words", align_bytes=MX_ALIGN)
         w_plane = sb.tile([P, Q], U8, name="w_plane", align_bytes=MX_ALIGN)
@@ -143,7 +148,7 @@ def tile_attend_pqkeys_kernel(tc, book_words, book_scales, query, size, vals, of
 
         pieces = (
             (v_words_first[:, 0:QUARTER], v_plane_first[:, 0:QUARTER], 0, QUARTER, nc.scalar.copy, nc.sync),
-            (v_words_first[:, QUARTER:HALF], v_plane_first[:, QUARTER:HALF], QUARTER, QUARTER, nc.vector.tensor_copy, nc.sync),
+            (v_words_next[:], v_plane_first[:, QUARTER:HALF], QUARTER, QUARTER, nc.vector.tensor_copy, nc.sync),
             (v_words_second[:, 0:QUARTER], v_plane_second[:, 0:QUARTER], HALF, QUARTER, nc.scalar.copy, nc.scalar),
             (v_words_second[:, QUARTER:HALF], v_plane_second[:, QUARTER:HALF], HALF + QUARTER, QUARTER, nc.vector.tensor_copy, nc.sync),
         )

@@ -12,7 +12,6 @@ U8 = mybir.dt.uint8
 FP8X4 = mybir.dt.float8_e4m3fn_x4
 ALU = mybir.AluOpType
 ACT = mybir.ActivationFunctionType
-AXIS = mybir.AxisListType
 
 P = 128
 PACK = 4
@@ -20,6 +19,7 @@ BLOCK_ROWS = 8
 QUADRANT = 32
 GROUP = 16
 D, C, I, Q, E = 512, 1024, 512, 128, 512
+SLOTS = I // 2
 HALF = E // 2
 QUARTER = E // 4
 MX_ALIGN = 64
@@ -32,22 +32,21 @@ def tile_attend_pqkeys_kernel(tc, book_words, book_scales, query, size, vals, of
         sb = ctx.enter_context(tc.tile_pool(name="sb", bufs=1))
         ps = ctx.enter_context(tc.psum_pool(name="ps", bufs=1))
 
-        scale_win = sb.tile([P, C], U8, name="scale_win", tag="scales_then_values", align_bytes=MX_ALIGN)
+        scale_win = sb.tile([P, C], U8, name="scale_win", tag="scales_values_sum", align_bytes=MX_ALIGN)
         nc.sync.dma_start(
             out=scale_win[:].bitcast(I32),
             in_=book_scales[0].bitcast(I32).unsqueeze(1).to_broadcast([P // BLOCK_ROWS, BLOCK_ROWS, C // 4]),
         )
         offsets = sb.tile([P, I // GROUP], U16, name="offsets")
         nc.sync.dma_start(offsets[:], offs)
-        word_win = sb.tile([P, C], I32, name="word_win", tag="words_then_values", align_bytes=MX_ALIGN)
+        word_win = sb.tile([P, C], I32, name="word_win", align_bytes=MX_ALIGN)
         nc.sync.dma_start(out=word_win[:], in_=book_words[0].rearrange("p c r -> p (c r)").bitcast(I32))
-        q_raw = sb.tile([P, PACK, Q], F32, name="q_raw")
-        nc.sync.dma_start(out=q_raw[:], in_=query.rearrange("(p t) q -> p t q", t=PACK))
         v_rows = vals.rearrange("(p t) e -> p t e", t=PACK)
-        v_raw_first = sb.tile([P, PACK, QUARTER], F32, name="v_raw_first")
-        nc.sync.dma_start(out=v_raw_first[:], in_=v_rows[:, :, 0:QUARTER])
         size_col = sb.tile([P, PACK], F32, name="size_col")
         nc.scalar.dma_start(out=size_col[:], in_=size.rearrange("o (p t) -> (o p) t", t=PACK))
+
+        q_raw = sb.tile([P, PACK, Q], F32, name="q_raw", tag="queries_then_values")
+        nc.scalar.dma_start(out=q_raw[:], in_=query.rearrange("(p t) q -> p t q", t=PACK))
 
         ident = sb.tile([P, P], F32, name="ident")
         zero = sb.tile([P, 1], F32, name="zero")
@@ -55,65 +54,84 @@ def tile_attend_pqkeys_kernel(tc, book_words, book_scales, query, size, vals, of
         nc.scalar.copy(ident[:], zero[:].to_broadcast([P, P]))
         make_identity(nc, ident[:], nomemset=True)
 
-        key_plane = sb.tile([P, I], U8, name="key_plane", align_bytes=MX_ALIGN)
-        nc.vector.memset(key_plane[:].bitcast(I32), 0)
-        got_scales = sb.tile([P, I], U8, name="got_scales", align_bytes=MX_ALIGN)
-        nc.vector.tensor_copy(got_scales[:], scale_win[:].indirect(offsets[:]))
-        for j in range(QUADRANT // BLOCK_ROWS):
-            (nc.sync, nc.scalar)[j % 2].dma_start(
-                out=key_plane[:].bitcast(I32)[j:P:QUADRANT, :],
-                in_=got_scales[:].bitcast(I32)[BLOCK_ROWS * j : P : QUADRANT, :],
-            )
-        v_raw_next = sb.tile([P, PACK, QUARTER], F32, name="v_raw_next", tag="scales_then_values", align_bytes=MX_ALIGN)
-        nc.sync.dma_start(out=v_raw_next[:], in_=v_rows[:, :, QUARTER:HALF])
-        key_words = sb.tile([P, I], U32, name="key_words", align_bytes=MX_ALIGN)
-        nc.vector.tensor_copy(key_words[:], word_win[:].bitcast(U32).indirect(offsets[:]))
-        v_raw_second = sb.tile([P, PACK, HALF], F32, name="v_raw_second", tag="words_then_values", align_bytes=MX_ALIGN)
-        nc.sync.dma_start(out=v_raw_second[:], in_=v_rows[:, :, HALF:E])
-
-        q_bf = sb.tile([P, Q, PACK], BF16, name="q_bf", align_bytes=MX_ALIGN)
-        nc.scalar.copy(q_bf[:], q_raw[:].rearrange("p t q -> p q t"))
-        q_words = sb.tile([P, Q], U32, name="q_words", tag="queries_then_values", align_bytes=MX_ALIGN)
-        q_plane = sb.tile([P, Q], U8, name="q_plane", align_bytes=MX_ALIGN)
-        nc.vector.quantize_mx(q_words[:].bitcast(FP8X4), q_plane[:], q_bf[:].rearrange("p q t -> p (q t)"))
-
-        size_ps = ps.tile([P, PACK, P], F32, name="size_ps")
-        for t in range(PACK):
-            nc.tensor.transpose(size_ps[:, t, :], size_col[:, t : t + 1].to_broadcast([P, P]), ident[:])
-
         def interleave(copy, dst, src):
             copy(dst.rearrange("p (c n) t -> p c t n", n=4), src.rearrange("p t (c n) -> p c t n", n=4))
 
         def quantise_values(words, plane, src):
             nc.vector.quantize_mx(words.bitcast(FP8X4), plane, src.rearrange("p e t -> p (e t)"))
 
-        v_bf_first = sb.tile([P, QUARTER, PACK], BF16, name="v_bf_first", align_bytes=MX_ALIGN)
-        interleave(nc.scalar.copy, v_bf_first[:], v_raw_first[:])
+        q_bf = sb.tile([P, Q, PACK], BF16, name="q_bf", align_bytes=MX_ALIGN)
+        interleave(nc.scalar.copy, q_bf[:], q_raw[:])
 
-        scores = ps.tile([P, I], F32, name="scores")
-        nc.tensor.matmul_mx(
-            scores[:], lhsT=q_words[:].bitcast(FP8X4), lhsT_scale=q_plane[:],
-            rhs=key_words[:].bitcast(FP8X4), rhs_scale=key_plane[:], start=True, stop=True,
-        )
-        neg_max = sb.tile([P, 1], F32, name="neg_max", tag="max_then_values", align_bytes=MX_ALIGN)
-        nc.vector.tensor_reduce(neg_max[:], scores[:], AXIS.X, ALU.max, negate=True)
+        halves = [slice(h * SLOTS // GROUP, (h + 1) * SLOTS // GROUP) for h in range(2)]
+        key_planes = []
+        for h in range(2):
+            key_plane = sb.tile([P, SLOTS], U8, name="key_plane%d" % h, align_bytes=MX_ALIGN)
+            nc.vector.memset(key_plane[:].bitcast(I32), 0)
+            got_scales = sb.tile([P, SLOTS], U8, name="got_scales%d" % h, align_bytes=MX_ALIGN)
+            nc.vector.tensor_copy(got_scales[:], scale_win[:].indirect(offsets[:, halves[h]]))
+            for j in range(QUADRANT // BLOCK_ROWS):
+                (nc.sync, nc.scalar)[j % 2].dma_start(
+                    out=key_plane[:].bitcast(I32)[j:P:QUADRANT, :],
+                    in_=got_scales[:].bitcast(I32)[BLOCK_ROWS * j : P : QUADRANT, :],
+                )
+            key_planes.append(key_plane)
+        v_raw_first = sb.tile([P, PACK, QUARTER], F32, name="v_raw_first", tag="scales_values_sum", align_bytes=MX_ALIGN)
+        nc.sync.dma_start(out=v_raw_first[:], in_=v_rows[:, :, 0:QUARTER])
+        q_words = sb.tile([P, Q], U32, name="q_words", align_bytes=MX_ALIGN)
+        q_plane = sb.tile([P, Q], U8, name="q_plane", align_bytes=MX_ALIGN)
+        nc.vector.quantize_mx(q_words[:].bitcast(FP8X4), q_plane[:], q_bf[:].rearrange("p q t -> p (q t)"))
+
+        key_words = []
+        for h in range(2):
+            words = sb.tile([P, SLOTS], U32, name="key_words%d" % h, tag="keys%d_then_values" % h, align_bytes=MX_ALIGN)
+            nc.vector.tensor_copy(words[:], word_win[:].bitcast(U32).indirect(offsets[:, halves[h]]))
+            key_words.append(words)
+        v_raw = sb.tile([P, PACK * (E - QUARTER)], F32, name="v_raw", tag="queries_then_values")
+        v_parts = [v_raw_first[:]]
+        for first, last in ((QUARTER, QUARTER + HALF), (QUARTER + HALF, E)):
+            part = v_raw[:, PACK * (first - QUARTER) : PACK * (last - QUARTER)].rearrange("p (t e) -> p t e", t=PACK)
+            nc.sync.dma_start(out=part, in_=v_rows[:, :, first:last])
+            v_parts.append(part)
+
+        negated = sb.tile([P, 2, P, 2], F32, name="negated", tag="scores_then_values", align_bytes=MX_ALIGN)
+        neg_max = [None]
+        for h in range(2):
+            scores = ps.tile([P, SLOTS], F32, name="scores%d" % h, tag="bank%d" % h)
+            nc.tensor.matmul_mx(
+                scores[:], lhsT=q_words[:].bitcast(FP8X4), lhsT_scale=q_plane[:],
+                rhs=key_words[h][:].bitcast(FP8X4), rhs_scale=key_planes[h][:], start=True, stop=True,
+            )
+            running = sb.tile([P, 1], F32, name="neg_max%d" % h)
+            nc.vector.tensor_scalar(
+                negated[:, :, h * P // 2 : (h + 1) * P // 2, :],
+                scores[:].rearrange("q (s u r) -> q u s r", u=2, r=2),
+                -1.0, neg_max[h], ALU.mult, ALU.min, accum_out=running[:],
+            )
+            neg_max.append(running[:])
+
+        size_ps = ps.tile([P, PACK, P], F32, name="size_ps", tag="bank0")
+        for t in range(PACK):
+            nc.tensor.transpose(size_ps[:, t, :], size_col[:, t : t + 1].to_broadcast([P, P]), ident[:])
+
         probs = sb.tile([P, 2, P, 2], F32, name="probs", tag="probs_then_values", align_bytes=MX_ALIGN)
         row_sum = sb.tile([P, 1], F32, name="row_sum")
-        nc.scalar.activation(
-            probs[:], scores[:].rearrange("q (s u r) -> q u s r", u=2, r=2), ACT.Exp,
-            bias=neg_max[:], accum_out=row_sum[:],
-        )
+        nc.scalar.activation(probs[:], negated[:], ACT.Exp, bias=neg_max[2], scale=-1.0, accum_out=row_sum[:])
 
-        v_words_first = sb.tile([P, QUARTER], U32, name="v_words_first", tag="queries_then_values", align_bytes=MX_ALIGN)
-        v_plane_first = sb.tile([P, HALF], U8, name="v_plane_first", align_bytes=MX_ALIGN)
-        quantise_values(v_words_first[:, 0:QUARTER], v_plane_first[:, 0:QUARTER], v_bf_first[:])
-        v_bf_late = sb.tile([P, 2, QUARTER, PACK], BF16, name="v_bf_late", tag="max_then_values", align_bytes=MX_ALIGN)
-        interleave(nc.scalar.copy, v_bf_late[:, 0], v_raw_next[:])
-        interleave(nc.scalar.copy, v_bf_late[:, 1], v_raw_second[:, :, QUARTER:HALF])
+        v_bf = [
+            sb.tile([P, QUARTER, PACK], BF16, name="v_bf0", tag="keys1_then_values", align_bytes=MX_ALIGN),
+            None, None, None,
+        ]
+        v_words = [None, sb.tile([P, QUARTER], U32, name="v_words1", align_bytes=MX_ALIGN)]
+        v_planes = [sb.tile([P, QUARTER], U8, name="v_plane%d" % n, align_bytes=MX_ALIGN) for n in range(4)]
+        interleave(nc.vector.tensor_copy, v_bf[0][:], v_parts[0])
+        v_bf_late = sb.tile([P, 2, QUARTER, PACK], BF16, name="v_bf_late", tag="scores_then_values", align_bytes=MX_ALIGN)
+        interleave(nc.scalar.copy, v_bf_late[:, 0], v_parts[1][:, :, 0:QUARTER])
+        interleave(nc.scalar.copy, v_bf_late[:, 1], v_parts[1][:, :, QUARTER:HALF])
 
-        inv_sum = sb.tile([P, 1], F32, name="inv_sum")
+        inv_sum = sb.tile([P, 1], F32, name="inv_sum", tag="scales_values_sum", align_bytes=MX_ALIGN)
         nc.vector.reciprocal(inv_sum[:], row_sum[:])
-        turned = ps.tile([P, 2, Q], F32, name="turned")
+        turned = ps.tile([P, 2, Q], F32, name="turned", tag="bank1")
         w_pairs = [sb.tile([P, P, 2], BF16, name="w_pair%d" % u) for u in range(2)]
         size_pairs = [size_ps[:, 2 * u : 2 * u + 2, :].rearrange("q r s -> q s r") for u in range(2)]
         sized = sb.tile([P, P, 2], F32, name="sized", tag="sized_then_values", align_bytes=MX_ALIGN)
@@ -127,14 +145,11 @@ def tile_attend_pqkeys_kernel(tc, book_words, book_scales, query, size, vals, of
                 turned[:, u, :], w_pairs[u][:].rearrange("q s r -> q (s r)").bitcast(F32), ident[:]
             )
 
-        v_bf_third = sb.tile([P, QUARTER, PACK], BF16, name="v_bf_third", tag="probs_then_values", align_bytes=MX_ALIGN)
-        interleave(nc.vector.tensor_copy, v_bf_third[:], v_raw_second[:, :, 0:QUARTER])
-        v_words_second = sb.tile([P, HALF], U32, name="v_words_second", align_bytes=MX_ALIGN)
-        v_plane_second = sb.tile([P, HALF], U8, name="v_plane_second", align_bytes=MX_ALIGN)
-        v_words_next = sb.tile([P, QUARTER], U32, name="v_words_next", tag="sized_then_values", align_bytes=MX_ALIGN)
-        quantise_values(v_words_next[:], v_plane_first[:, QUARTER:HALF], v_bf_late[:, 0])
-        quantise_values(v_words_second[:, 0:QUARTER], v_plane_second[:, 0:QUARTER], v_bf_third[:])
-        quantise_values(v_words_second[:, QUARTER:HALF], v_plane_second[:, QUARTER:HALF], v_bf_late[:, 1])
+        v_bf_last = sb.tile([P, QUARTER, PACK], BF16, name="v_bf_last", tag="sized_then_values", align_bytes=MX_ALIGN)
+        v_words[0] = sb.tile([P, QUARTER], U32, name="v_words0", tag="probs_then_values", align_bytes=MX_ALIGN)
+        quantise_values(v_words[0][:], v_planes[0][:], v_bf[0][:])
+        interleave(nc.vector.tensor_copy, v_bf_last[:], v_parts[2])
+        quantise_values(v_words[1][:], v_planes[1][:], v_bf_late[:, 0])
 
         w_words = sb.tile([P, Q], U32, name="w_words", align_bytes=MX_ALIGN)
         w_plane = sb.tile([P, Q], U8, name="w_plane", align_bytes=MX_ALIGN)
@@ -145,19 +160,19 @@ def tile_attend_pqkeys_kernel(tc, book_words, book_scales, query, size, vals, of
                 turned[:, :, rows].rearrange("s u q -> s q u"),
             )
             nc.vector.quantize_mx(w_words[:, rows].bitcast(FP8X4), w_plane[:, rows], wt_bf[:])
+        for n, src in ((2, v_bf_late[:, 1]), (3, v_bf_last[:])):
+            words = sb.tile([P, QUARTER], U32, name="v_words%d" % n, tag="wt_bf%d" % ((n - 2) * Q // 2), align_bytes=MX_ALIGN)
+            quantise_values(words[:], v_planes[n][:], src)
+            v_words.append(words)
 
-        pieces = (
-            (v_words_first[:, 0:QUARTER], v_plane_first[:, 0:QUARTER], 0, QUARTER, nc.scalar.copy, nc.sync),
-            (v_words_next[:], v_plane_first[:, QUARTER:HALF], QUARTER, QUARTER, nc.vector.tensor_copy, nc.sync),
-            (v_words_second[:, 0:QUARTER], v_plane_second[:, 0:QUARTER], HALF, QUARTER, nc.scalar.copy, nc.scalar),
-            (v_words_second[:, QUARTER:HALF], v_plane_second[:, QUARTER:HALF], HALF + QUARTER, QUARTER, nc.vector.tensor_copy, nc.sync),
-        )
-        for n, (words, plane, first, width, copy, queue) in enumerate(pieces):
-            acc = ps.tile([P, width], F32, name="acc%d" % n)
+        copies = (nc.scalar.copy, nc.vector.tensor_copy)
+        queues = (nc.sync, nc.sync, nc.scalar, nc.sync)
+        for n in range(4):
+            acc = ps.tile([P, QUARTER], F32, name="acc%d" % n)
             nc.tensor.matmul_mx(
                 acc[:], lhsT=w_words[:].bitcast(FP8X4), lhsT_scale=w_plane[:],
-                rhs=words.bitcast(FP8X4), rhs_scale=plane, start=True, stop=True,
+                rhs=v_words[n][:].bitcast(FP8X4), rhs_scale=v_planes[n][:], start=True, stop=True,
             )
-            res = sb.tile([P, width], F32, name="res%d" % n)
-            copy(res[:], acc[:])
-            queue.dma_start(out=out[:, first : first + width], in_=res[:])
+            res = sb.tile([P, QUARTER], F32, name="res%d" % n)
+            copies[n % 2](res[:], acc[:])
+            queues[n].dma_start(out=out[:, n * QUARTER : (n + 1) * QUARTER], in_=res[:])

@@ -1,7 +1,6 @@
 from contextlib import ExitStack
 
 import concourse.mybir as mybir
-from concourse.masks import make_identity
 
 F32 = mybir.dt.float32
 BF16 = mybir.dt.bfloat16
@@ -39,20 +38,35 @@ def tile_attend_pqkeys_kernel(tc, book_words, book_scales, query, size, vals, of
         )
         offsets = sb.tile([P, I // GROUP], U16, name="offsets")
         nc.sync.dma_start(offsets[:], offs)
-        word_win = sb.tile([P, C], I32, name="word_win", align_bytes=MX_ALIGN)
-        nc.sync.dma_start(out=word_win[:], in_=book_words[0].rearrange("p c r -> p (c r)").bitcast(I32))
         v_rows = vals.rearrange("(p t) e -> p t e", t=PACK)
         size_col = sb.tile([P, PACK], F32, name="size_col")
         nc.scalar.dma_start(out=size_col[:], in_=size.rearrange("o (p t) -> (o p) t", t=PACK))
 
         q_raw = sb.tile([P, PACK, Q], F32, name="q_raw", tag="queries_then_values")
         nc.scalar.dma_start(out=q_raw[:], in_=query.rearrange("(p t) q -> p t q", t=PACK))
+        word_win = sb.tile([P, C], I32, name="word_win", align_bytes=MX_ALIGN)
+        nc.scalar.dma_start(out=word_win[:], in_=book_words[0].rearrange("p c r -> p (c r)").bitcast(I32))
 
+        one = sb.tile([P, 1], F32, name="one")
+        nc.vector.memset(one[:], 1.0)
+        base = sb.tile([P, 1], F32, name="base")
+        for first in range(0, P, QUADRANT):
+            nc.gpsimd.memset(base[first : first + QUADRANT, :], float(first))
+        col = sb.tile([P, P], F32, name="col")
+        ones = one[:].to_broadcast([P, P])
+        nc.vector.tensor_tensor_scan(col[:], ones, ones, 0.0, ALU.mult, ALU.add)
+        from_base = sb.tile([P, QUADRANT], F32, name="from_base", align_bytes=MX_ALIGN)
+        nc.vector.tensor_scalar(from_base[:], col[:, 0:QUADRANT], base[:], None, ALU.add)
+        row = sb.tile([P, QUADRANT], F32, name="row", align_bytes=MX_ALIGN)
+        nc.vector.transpose(row[:], from_base[:])
+        off_diagonal = sb.tile([P, P], F32, name="off_diagonal")
+        nc.vector.tensor_scalar(off_diagonal[:], col[:], row[:, 0:1], None, ALU.not_equal)
         ident = sb.tile([P, P], F32, name="ident")
-        zero = sb.tile([P, 1], F32, name="zero")
-        nc.vector.memset(zero[:], 0.0)
-        nc.scalar.copy(ident[:], zero[:].to_broadcast([P, P]))
-        make_identity(nc, ident[:], nomemset=True)
+        nc.scalar.activation(ident[:], off_diagonal[:], ACT.Copy, bias=1.0, scale=-1.0)
+
+        size_ps = ps.tile([P, PACK, P], F32, name="size_ps")
+        for t in range(PACK):
+            nc.tensor.transpose(size_ps[:, t, :], size_col[:, t : t + 1].to_broadcast([P, P]), ident[:])
 
         def interleave(copy, dst, src):
             copy(dst.rearrange("p (c n) t -> p c t n", n=4), src.rearrange("p t (c n) -> p c t n", n=4))
@@ -64,6 +78,7 @@ def tile_attend_pqkeys_kernel(tc, book_words, book_scales, query, size, vals, of
         interleave(nc.scalar.copy, q_bf[:], q_raw[:])
 
         halves = [slice(h * SLOTS // GROUP, (h + 1) * SLOTS // GROUP) for h in range(2)]
+        move_queues = ((nc.sync, nc.sync, nc.scalar, nc.sync), (nc.sync, nc.scalar, nc.sync, nc.scalar))
         key_planes = []
         for h in range(2):
             key_plane = sb.tile([P, SLOTS], U8, name="key_plane%d" % h, align_bytes=MX_ALIGN)
@@ -71,28 +86,24 @@ def tile_attend_pqkeys_kernel(tc, book_words, book_scales, query, size, vals, of
             got_scales = sb.tile([P, SLOTS], U8, name="got_scales%d" % h, align_bytes=MX_ALIGN)
             nc.vector.tensor_copy(got_scales[:], scale_win[:].indirect(offsets[:, halves[h]]))
             for j in range(QUADRANT // BLOCK_ROWS):
-                (nc.sync, nc.scalar)[j % 2].dma_start(
+                move_queues[h][j].dma_start(
                     out=key_plane[:].bitcast(I32)[j:P:QUADRANT, :],
                     in_=got_scales[:].bitcast(I32)[BLOCK_ROWS * j : P : QUADRANT, :],
                 )
             key_planes.append(key_plane)
-        v_raw_first = sb.tile([P, PACK, QUARTER], F32, name="v_raw_first", tag="scales_values_sum", align_bytes=MX_ALIGN)
-        nc.sync.dma_start(out=v_raw_first[:], in_=v_rows[:, :, 0:QUARTER])
+        v_raw_first = sb.tile([P, PACK, HALF], F32, name="v_raw_first", tag="scales_values_sum", align_bytes=MX_ALIGN)
+        nc.scalar.dma_start(out=v_raw_first[:], in_=v_rows[:, :, 0:HALF])
         q_words = sb.tile([P, Q], U32, name="q_words", align_bytes=MX_ALIGN)
         q_plane = sb.tile([P, Q], U8, name="q_plane", align_bytes=MX_ALIGN)
         nc.vector.quantize_mx(q_words[:].bitcast(FP8X4), q_plane[:], q_bf[:].rearrange("p q t -> p (q t)"))
 
         key_words = []
         for h in range(2):
-            words = sb.tile([P, SLOTS], U32, name="key_words%d" % h, tag="keys%d_then_values" % h, align_bytes=MX_ALIGN)
+            words = sb.tile([P, SLOTS], U32, name="key_words%d" % h, align_bytes=MX_ALIGN)
             nc.vector.tensor_copy(words[:], word_win[:].bitcast(U32).indirect(offsets[:, halves[h]]))
             key_words.append(words)
-        v_raw = sb.tile([P, PACK * (E - QUARTER)], F32, name="v_raw", tag="queries_then_values")
-        v_parts = [v_raw_first[:]]
-        for first, last in ((QUARTER, QUARTER + HALF), (QUARTER + HALF, E)):
-            part = v_raw[:, PACK * (first - QUARTER) : PACK * (last - QUARTER)].rearrange("p (t e) -> p t e", t=PACK)
-            nc.sync.dma_start(out=part, in_=v_rows[:, :, first:last])
-            v_parts.append(part)
+        v_raw_second = sb.tile([P, PACK, HALF], F32, name="v_raw_second", tag="queries_then_values")
+        nc.scalar.dma_start(out=v_raw_second[:], in_=v_rows[:, :, HALF:E])
 
         negated = sb.tile([P, 2, P, 2], F32, name="negated", tag="scores_then_values", align_bytes=MX_ALIGN)
         neg_max = [None]
@@ -110,26 +121,16 @@ def tile_attend_pqkeys_kernel(tc, book_words, book_scales, query, size, vals, of
             )
             neg_max.append(running[:])
 
-        size_ps = ps.tile([P, PACK, P], F32, name="size_ps", tag="bank0")
-        for t in range(PACK):
-            nc.tensor.transpose(size_ps[:, t, :], size_col[:, t : t + 1].to_broadcast([P, P]), ident[:])
-
         probs = sb.tile([P, 2, P, 2], F32, name="probs", tag="probs_then_values", align_bytes=MX_ALIGN)
         row_sum = sb.tile([P, 1], F32, name="row_sum")
         nc.scalar.activation(probs[:], negated[:], ACT.Exp, bias=neg_max[2], scale=-1.0, accum_out=row_sum[:])
 
-        v_bf = [
-            sb.tile([P, QUARTER, PACK], BF16, name="v_bf0", tag="keys1_then_values", align_bytes=MX_ALIGN),
-            None, None, None,
-        ]
-        v_words = [None, sb.tile([P, QUARTER], U32, name="v_words1", align_bytes=MX_ALIGN)]
         v_planes = [sb.tile([P, QUARTER], U8, name="v_plane%d" % n, align_bytes=MX_ALIGN) for n in range(4)]
-        interleave(nc.vector.tensor_copy, v_bf[0][:], v_parts[0])
-        v_bf_late = sb.tile([P, 2, QUARTER, PACK], BF16, name="v_bf_late", tag="scores_then_values", align_bytes=MX_ALIGN)
-        interleave(nc.scalar.copy, v_bf_late[:, 0], v_parts[1][:, :, 0:QUARTER])
-        interleave(nc.scalar.copy, v_bf_late[:, 1], v_parts[1][:, :, QUARTER:HALF])
+        v_bf_first = sb.tile([P, 2, QUARTER, PACK], BF16, name="v_bf_first", tag="scores_then_values", align_bytes=MX_ALIGN)
+        for n in range(2):
+            interleave(nc.scalar.copy, v_bf_first[:, n], v_raw_first[:, :, n * QUARTER : (n + 1) * QUARTER])
 
-        inv_sum = sb.tile([P, 1], F32, name="inv_sum", tag="scales_values_sum", align_bytes=MX_ALIGN)
+        inv_sum = sb.tile([P, 1], F32, name="inv_sum")
         nc.vector.reciprocal(inv_sum[:], row_sum[:])
         turned = ps.tile([P, 2, Q], F32, name="turned", tag="bank1")
         w_pairs = [sb.tile([P, P, 2], BF16, name="w_pair%d" % u) for u in range(2)]
@@ -145,11 +146,12 @@ def tile_attend_pqkeys_kernel(tc, book_words, book_scales, query, size, vals, of
                 turned[:, u, :], w_pairs[u][:].rearrange("q s r -> q (s r)").bitcast(F32), ident[:]
             )
 
-        v_bf_last = sb.tile([P, QUARTER, PACK], BF16, name="v_bf_last", tag="sized_then_values", align_bytes=MX_ALIGN)
-        v_words[0] = sb.tile([P, QUARTER], U32, name="v_words0", tag="probs_then_values", align_bytes=MX_ALIGN)
-        quantise_values(v_words[0][:], v_planes[0][:], v_bf[0][:])
-        interleave(nc.vector.tensor_copy, v_bf_last[:], v_parts[2])
-        quantise_values(v_words[1][:], v_planes[1][:], v_bf_late[:, 0])
+        v_bf_second = sb.tile([P, HALF, PACK], BF16, name="v_bf_second", tag="sized_then_values", align_bytes=MX_ALIGN)
+        v_words_first = sb.tile([P, HALF], U32, name="v_words_first", tag="probs_then_values", align_bytes=MX_ALIGN)
+        v_words = [v_words_first[:, 0:QUARTER], v_words_first[:, QUARTER:HALF]]
+        quantise_values(v_words[0], v_planes[0][:], v_bf_first[:, 0])
+        interleave(nc.vector.tensor_copy, v_bf_second[:], v_raw_second[:])
+        quantise_values(v_words[1], v_planes[1][:], v_bf_first[:, 1])
 
         w_words = sb.tile([P, Q], U32, name="w_words", align_bytes=MX_ALIGN)
         w_plane = sb.tile([P, Q], U8, name="w_plane", align_bytes=MX_ALIGN)
@@ -160,10 +162,10 @@ def tile_attend_pqkeys_kernel(tc, book_words, book_scales, query, size, vals, of
                 turned[:, :, rows].rearrange("s u q -> s q u"),
             )
             nc.vector.quantize_mx(w_words[:, rows].bitcast(FP8X4), w_plane[:, rows], wt_bf[:])
-        for n, src in ((2, v_bf_late[:, 1]), (3, v_bf_last[:])):
+        for n, src in ((2, v_bf_second[:, 0:QUARTER]), (3, v_bf_second[:, QUARTER:HALF])):
             words = sb.tile([P, QUARTER], U32, name="v_words%d" % n, tag="wt_bf%d" % ((n - 2) * Q // 2), align_bytes=MX_ALIGN)
             quantise_values(words[:], v_planes[n][:], src)
-            v_words.append(words)
+            v_words.append(words[:])
 
         copies = (nc.scalar.copy, nc.vector.tensor_copy)
         queues = (nc.sync, nc.sync, nc.scalar, nc.sync)
@@ -171,7 +173,7 @@ def tile_attend_pqkeys_kernel(tc, book_words, book_scales, query, size, vals, of
             acc = ps.tile([P, QUARTER], F32, name="acc%d" % n)
             nc.tensor.matmul_mx(
                 acc[:], lhsT=w_words[:].bitcast(FP8X4), lhsT_scale=w_plane[:],
-                rhs=v_words[n][:].bitcast(FP8X4), rhs_scale=v_planes[n][:], start=True, stop=True,
+                rhs=v_words[n].bitcast(FP8X4), rhs_scale=v_planes[n][:], start=True, stop=True,
             )
             res = sb.tile([P, QUARTER], F32, name="res%d" % n)
             copies[n % 2](res[:], acc[:])

@@ -11,6 +11,7 @@ U8 = mybir.dt.uint8
 FP8X4 = mybir.dt.float8_e4m3fn_x4
 ALU = mybir.AluOpType
 ACT = mybir.ActivationFunctionType
+AXIS = mybir.AxisListType
 
 P = 128
 PACK = 4
@@ -52,15 +53,13 @@ def tile_attend_pqkeys_kernel(tc, book_words, book_scales, query, size, vals, of
         base = sb.tile([P, 1], F32, name="base")
         for first in range(0, P, QUADRANT):
             nc.gpsimd.memset(base[first : first + QUADRANT, :], float(first))
-        col = sb.tile([P, P], F32, name="col")
+        col = sb.tile([P, P], F32, name="col", align_bytes=MX_ALIGN)
         ones = one[:].to_broadcast([P, P])
         nc.vector.tensor_tensor_scan(col[:], ones, ones, 0.0, ALU.mult, ALU.add)
-        from_base = sb.tile([P, QUADRANT], F32, name="from_base", align_bytes=MX_ALIGN)
-        nc.vector.tensor_scalar(from_base[:], col[:, 0:QUADRANT], base[:], None, ALU.add)
         row = sb.tile([P, QUADRANT], F32, name="row", align_bytes=MX_ALIGN)
-        nc.vector.transpose(row[:], from_base[:])
+        nc.vector.transpose(row[:], col[:, 0:QUADRANT])
         off_diagonal = sb.tile([P, P], F32, name="off_diagonal")
-        nc.vector.tensor_scalar(off_diagonal[:], col[:], row[:, 0:1], None, ALU.not_equal)
+        nc.vector.tensor_scalar(off_diagonal[:], col[:], base[:], row[:, 0:1], ALU.subtract, ALU.not_equal)
         ident = sb.tile([P, P], F32, name="ident")
         nc.scalar.activation(ident[:], off_diagonal[:], ACT.Copy, bias=1.0, scale=-1.0)
 
@@ -105,49 +104,57 @@ def tile_attend_pqkeys_kernel(tc, book_words, book_scales, query, size, vals, of
         v_raw_second = sb.tile([P, PACK, HALF], F32, name="v_raw_second", tag="queries_then_values")
         nc.scalar.dma_start(out=v_raw_second[:], in_=v_rows[:, :, HALF:E])
 
-        negated = sb.tile([P, 2, P, 2], F32, name="negated", tag="scores_then_values", align_bytes=MX_ALIGN)
-        neg_max = [None]
+        def by_pairs(row):
+            return row.rearrange("q (s u r) -> q u s r", u=2, r=2)
+
+        scores = []
         for h in range(2):
-            scores = ps.tile([P, SLOTS], F32, name="scores%d" % h, tag="bank%d" % h)
+            bank = ps.tile([P, SLOTS], F32, name="scores%d" % h, tag="bank%d" % h)
             nc.tensor.matmul_mx(
-                scores[:], lhsT=q_words[:].bitcast(FP8X4), lhsT_scale=q_plane[:],
+                bank[:], lhsT=q_words[:].bitcast(FP8X4), lhsT_scale=q_plane[:],
                 rhs=key_words[h][:].bitcast(FP8X4), rhs_scale=key_planes[h][:], start=True, stop=True,
             )
-            running = sb.tile([P, 1], F32, name="neg_max%d" % h)
-            nc.vector.tensor_scalar(
-                negated[:, :, h * P // 2 : (h + 1) * P // 2, :],
-                scores[:].rearrange("q (s u r) -> q u s r", u=2, r=2),
-                -1.0, neg_max[h], ALU.mult, ALU.min, accum_out=running[:],
-            )
-            neg_max.append(running[:])
-
-        probs = sb.tile([P, 2, P, 2], F32, name="probs", tag="probs_then_values", align_bytes=MX_ALIGN)
-        row_sum = sb.tile([P, 1], F32, name="row_sum")
-        nc.scalar.activation(probs[:], negated[:], ACT.Exp, bias=neg_max[2], scale=-1.0, accum_out=row_sum[:])
+            scores.append(bank[:])
+        probs = [sb.tile([P, 2, P // 2, 2], F32, name="probs%d" % h, align_bytes=MX_ALIGN) for h in range(2)]
+        sums = [sb.tile([P, 1], F32, name="sum%d" % h) for h in range(2)]
+        neg_first_max = sb.tile([P, 1], F32, name="neg_first_max")
+        nc.vector.tensor_reduce(neg_first_max[:], scores[0], AXIS.X, ALU.max, negate=True)
+        nc.scalar.activation(probs[0][:], by_pairs(scores[0]), ACT.Exp, bias=neg_first_max[:], accum_out=sums[0][:])
+        negated = sb.tile([P, 2, P // 2, 2], F32, name="negated", tag="scores_then_values", align_bytes=MX_ALIGN)
+        neg_max = sb.tile([P, 1], F32, name="neg_max")
+        nc.vector.tensor_scalar(
+            negated[:], by_pairs(scores[1]), -1.0, neg_first_max[:], ALU.mult, ALU.min, accum_out=neg_max[:]
+        )
+        shift = sb.tile([P, 1], F32, name="shift")
+        nc.scalar.activation(shift[:], neg_first_max[:], ACT.Exp, bias=neg_max[:], scale=-1.0)
+        nc.scalar.activation(probs[1][:], negated[:], ACT.Exp, bias=neg_max[:], scale=-1.0, accum_out=sums[1][:])
 
         v_planes = [sb.tile([P, QUARTER], U8, name="v_plane%d" % n, align_bytes=MX_ALIGN) for n in range(4)]
         v_bf_first = sb.tile([P, 2, QUARTER, PACK], BF16, name="v_bf_first", tag="scores_then_values", align_bytes=MX_ALIGN)
         for n in range(2):
             interleave(nc.scalar.copy, v_bf_first[:, n], v_raw_first[:, :, n * QUARTER : (n + 1) * QUARTER])
 
+        size_pairs = size_ps[:].rearrange("q (u r) s -> q u s r", u=2)
+        sized = [sb.tile([P, 2, P // 2, 2], F32, name="sized%d" % h, align_bytes=MX_ALIGN) for h in range(2)]
+        nc.vector.tensor_tensor(sized[0][:], probs[0][:], size_pairs[:, :, 0 : P // 2, :], ALU.mult)
+        row_sum = sb.tile([P, 1], F32, name="row_sum")
+        nc.vector.tensor_scalar(row_sum[:], sums[0][:], shift[:], sums[1][:], ALU.mult, ALU.add)
+        nc.vector.tensor_tensor(sized[1][:], probs[1][:], size_pairs[:, :, P // 2 : P, :], ALU.mult)
         inv_sum = sb.tile([P, 1], F32, name="inv_sum")
         nc.vector.reciprocal(inv_sum[:], row_sum[:])
         turned = ps.tile([P, 2, Q], F32, name="turned", tag="bank1")
-        w_pairs = [sb.tile([P, P, 2], BF16, name="w_pair%d" % u) for u in range(2)]
-        size_pairs = [size_ps[:, 2 * u : 2 * u + 2, :].rearrange("q r s -> q s r") for u in range(2)]
-        sized = sb.tile([P, P, 2], F32, name="sized", tag="sized_then_values", align_bytes=MX_ALIGN)
-        nc.vector.tensor_tensor(sized[:], probs[:, 1, :, :], size_pairs[1], ALU.mult)
-        nc.vector.scalar_tensor_tensor(
-            w_pairs[0][:], probs[:, 0, :, :], inv_sum[:], size_pairs[0], ALU.mult, ALU.mult
-        )
-        nc.vector.tensor_scalar(w_pairs[1][:], sized[:], inv_sum[:], None, ALU.mult)
         for u in range(2):
+            w_pair = sb.tile([P, P, 2], BF16, name="w_pair%d" % u)
+            nc.vector.tensor_scalar(
+                w_pair[:, 0 : P // 2, :], sized[0][:, u], shift[:], inv_sum[:], ALU.mult, ALU.mult
+            )
+            nc.vector.tensor_scalar(w_pair[:, P // 2 : P, :], sized[1][:, u], inv_sum[:], None, ALU.mult)
             nc.tensor.transpose(
-                turned[:, u, :], w_pairs[u][:].rearrange("q s r -> q (s r)").bitcast(F32), ident[:]
+                turned[:, u, :], w_pair[:].rearrange("q s r -> q (s r)").bitcast(F32), ident[:]
             )
 
-        v_bf_second = sb.tile([P, HALF, PACK], BF16, name="v_bf_second", tag="sized_then_values", align_bytes=MX_ALIGN)
-        v_words_first = sb.tile([P, HALF], U32, name="v_words_first", tag="probs_then_values", align_bytes=MX_ALIGN)
+        v_bf_second = sb.tile([P, HALF, PACK], BF16, name="v_bf_second", tag="sized1", align_bytes=MX_ALIGN)
+        v_words_first = sb.tile([P, HALF], U32, name="v_words_first", tag="sized0", align_bytes=MX_ALIGN)
         v_words = [v_words_first[:, 0:QUARTER], v_words_first[:, QUARTER:HALF]]
         quantise_values(v_words[0], v_planes[0][:], v_bf_first[:, 0])
         interleave(nc.vector.tensor_copy, v_bf_second[:], v_raw_second[:])

@@ -33,7 +33,7 @@ def tile_attend_pqkeys_kernel(tc, book_words, book_scales, query, size, vals, of
         ps = ctx.enter_context(tc.psum_pool(name="ps", bufs=1))
 
         scale_win = sb.tile([P, C], U8, name="scale_win", tag="scales_values_sum", align_bytes=MX_ALIGN)
-        nc.sync.dma_start(
+        nc.scalar.dma_start(
             out=scale_win[:].bitcast(I32),
             in_=book_scales[0].bitcast(I32).unsqueeze(1).to_broadcast([P // BLOCK_ROWS, BLOCK_ROWS, C // 4]),
         )
@@ -41,7 +41,7 @@ def tile_attend_pqkeys_kernel(tc, book_words, book_scales, query, size, vals, of
         nc.sync.dma_start(offsets[:], offs)
         v_rows = vals.rearrange("(p t) e -> p t e", t=PACK)
         size_col = sb.tile([P, PACK], F32, name="size_col")
-        nc.scalar.dma_start(out=size_col[:], in_=size.rearrange("o (p t) -> (o p) t", t=PACK))
+        nc.sync.dma_start(out=size_col[:], in_=size.rearrange("o (p t) -> (o p) t", t=PACK))
 
         q_raw = sb.tile([P, PACK, Q], F32, name="q_raw", tag="queries_then_values")
         nc.scalar.dma_start(out=q_raw[:], in_=query.rearrange("(p t) q -> p t q", t=PACK))
@@ -115,19 +115,25 @@ def tile_attend_pqkeys_kernel(tc, book_words, book_scales, query, size, vals, of
                 rhs=key_words[h][:].bitcast(FP8X4), rhs_scale=key_planes[h][:], start=True, stop=True,
             )
             scores.append(bank[:])
-        probs = [sb.tile([P, 2, P // 2, 2], F32, name="probs%d" % h, align_bytes=MX_ALIGN) for h in range(2)]
+        def paired(cols):
+            return cols.rearrange("q (u s r) -> q u s r", u=2, r=2)
+
+        probs_first = sb.tile([P, SLOTS], F32, name="probs_first", align_bytes=MX_ALIGN)
+        probs_second = sb.tile([P, SLOTS + 1], F32, name="probs_second", align_bytes=MX_ALIGN)
+        probs = [paired(probs_first[:]), paired(probs_second[:, 0:SLOTS])]
+        shift = probs_second[:, SLOTS : SLOTS + 1]
         sums = [sb.tile([P, 1], F32, name="sum%d" % h) for h in range(2)]
-        neg_first_max = sb.tile([P, 1], F32, name="neg_first_max")
-        nc.vector.tensor_reduce(neg_first_max[:], scores[0], AXIS.X, ALU.max, negate=True)
-        nc.scalar.activation(probs[0][:], by_pairs(scores[0]), ACT.Exp, bias=neg_first_max[:], accum_out=sums[0][:])
-        negated = sb.tile([P, 2, P // 2, 2], F32, name="negated", tag="scores_then_values", align_bytes=MX_ALIGN)
+        negated = sb.tile([P, SLOTS + 1], F32, name="negated", tag="scores_then_values", align_bytes=MX_ALIGN)
+        neg_first_max = negated[:, SLOTS : SLOTS + 1]
+        nc.vector.tensor_reduce(neg_first_max, scores[0], AXIS.X, ALU.max, negate=True)
+        nc.scalar.activation(probs[0], by_pairs(scores[0]), ACT.Exp, bias=neg_first_max, accum_out=sums[0][:])
         neg_max = sb.tile([P, 1], F32, name="neg_max")
         nc.vector.tensor_scalar(
-            negated[:], by_pairs(scores[1]), -1.0, neg_first_max[:], ALU.mult, ALU.min, accum_out=neg_max[:]
+            paired(negated[:, 0:SLOTS]), by_pairs(scores[1]), -1.0, neg_first_max, ALU.mult, ALU.min, accum_out=neg_max[:]
         )
-        shift = sb.tile([P, 1], F32, name="shift")
-        nc.scalar.activation(shift[:], neg_first_max[:], ACT.Exp, bias=neg_max[:], scale=-1.0)
-        nc.scalar.activation(probs[1][:], negated[:], ACT.Exp, bias=neg_max[:], scale=-1.0, accum_out=sums[1][:])
+        nc.scalar.activation(probs_second[:], negated[:], ACT.Exp, bias=neg_max[:], scale=-1.0, accum_out=sums[1][:])
+        first_sum_less_one = sb.tile([P, 1], F32, name="first_sum_less_one")
+        nc.vector.tensor_scalar(first_sum_less_one[:], sums[0][:], -1.0, None, ALU.add)
 
         v_planes = [sb.tile([P, QUARTER], U8, name="v_plane%d" % n, align_bytes=MX_ALIGN) for n in range(4)]
         v_bf_first = sb.tile([P, 2, QUARTER, PACK], BF16, name="v_bf_first", tag="scores_then_values", align_bytes=MX_ALIGN)
@@ -136,17 +142,17 @@ def tile_attend_pqkeys_kernel(tc, book_words, book_scales, query, size, vals, of
 
         size_pairs = size_ps[:].rearrange("q (u r) s -> q u s r", u=2)
         sized = [sb.tile([P, 2, P // 2, 2], F32, name="sized%d" % h, align_bytes=MX_ALIGN) for h in range(2)]
-        nc.vector.tensor_tensor(sized[0][:], probs[0][:], size_pairs[:, :, 0 : P // 2, :], ALU.mult)
+        nc.vector.tensor_tensor(sized[0][:], probs[0], size_pairs[:, :, 0 : P // 2, :], ALU.mult)
         row_sum = sb.tile([P, 1], F32, name="row_sum")
-        nc.vector.tensor_scalar(row_sum[:], sums[0][:], shift[:], sums[1][:], ALU.mult, ALU.add)
-        nc.vector.tensor_tensor(sized[1][:], probs[1][:], size_pairs[:, :, P // 2 : P, :], ALU.mult)
+        nc.vector.tensor_scalar(row_sum[:], first_sum_less_one[:], shift, sums[1][:], ALU.mult, ALU.add)
+        nc.vector.tensor_tensor(sized[1][:], probs[1], size_pairs[:, :, P // 2 : P, :], ALU.mult)
         inv_sum = sb.tile([P, 1], F32, name="inv_sum")
         nc.vector.reciprocal(inv_sum[:], row_sum[:])
         turned = ps.tile([P, 2, Q], F32, name="turned", tag="bank1")
         for u in range(2):
             w_pair = sb.tile([P, P, 2], BF16, name="w_pair%d" % u)
             nc.vector.tensor_scalar(
-                w_pair[:, 0 : P // 2, :], sized[0][:, u], shift[:], inv_sum[:], ALU.mult, ALU.mult
+                w_pair[:, 0 : P // 2, :], sized[0][:, u], shift, inv_sum[:], ALU.mult, ALU.mult
             )
             nc.vector.tensor_scalar(w_pair[:, P // 2 : P, :], sized[1][:, u], inv_sum[:], None, ALU.mult)
             nc.tensor.transpose(

@@ -90,8 +90,9 @@ def tile_attend_pqkeys_kernel(tc, book_words, book_scales, query, size, vals, of
                     in_=got_scales[:].bitcast(I32)[BLOCK_ROWS * j : P : QUADRANT, :],
                 )
             key_planes.append(key_plane)
-        v_raw_first = sb.tile([P, PACK, HALF], F32, name="v_raw_first", tag="scales_values_sum", align_bytes=MX_ALIGN)
-        nc.scalar.dma_start(out=v_raw_first[:], in_=v_rows[:, :, 0:HALF])
+        v_raw_first = sb.tile([P, 2, PACK, QUARTER], F32, name="v_raw_first", tag="scales_values_sum", align_bytes=MX_ALIGN)
+        for n in range(2):
+            nc.scalar.dma_start(out=v_raw_first[:, n], in_=v_rows[:, :, n * QUARTER : (n + 1) * QUARTER])
         q_words = sb.tile([P, Q], U32, name="q_words", align_bytes=MX_ALIGN)
         q_plane = sb.tile([P, Q], U8, name="q_plane", align_bytes=MX_ALIGN)
         nc.vector.quantize_mx(q_words[:].bitcast(FP8X4), q_plane[:], q_bf[:].rearrange("p q t -> p (q t)"))
@@ -101,8 +102,9 @@ def tile_attend_pqkeys_kernel(tc, book_words, book_scales, query, size, vals, of
             words = sb.tile([P, SLOTS], U32, name="key_words%d" % h, align_bytes=MX_ALIGN)
             nc.vector.tensor_copy(words[:], word_win[:].bitcast(U32).indirect(offsets[:, halves[h]]))
             key_words.append(words)
-        v_raw_second = sb.tile([P, PACK, HALF], F32, name="v_raw_second", tag="queries_then_values")
-        nc.scalar.dma_start(out=v_raw_second[:], in_=v_rows[:, :, HALF:E])
+        v_raw_second = sb.tile([P, 2, PACK, QUARTER], F32, name="v_raw_second", tag="queries_then_values")
+        for n in range(2):
+            nc.scalar.dma_start(out=v_raw_second[:, n], in_=v_rows[:, :, HALF + n * QUARTER : HALF + (n + 1) * QUARTER])
 
         def by_pairs(row):
             return row.rearrange("q (s u r) -> q u s r", u=2, r=2)
@@ -138,16 +140,17 @@ def tile_attend_pqkeys_kernel(tc, book_words, book_scales, query, size, vals, of
         v_planes = [sb.tile([P, QUARTER], U8, name="v_plane%d" % n, align_bytes=MX_ALIGN) for n in range(4)]
         v_bf_first = sb.tile([P, 2, QUARTER, PACK], BF16, name="v_bf_first", tag="scores_then_values", align_bytes=MX_ALIGN)
         for n in range(2):
-            interleave(nc.scalar.copy, v_bf_first[:, n], v_raw_first[:, :, n * QUARTER : (n + 1) * QUARTER])
+            interleave(nc.scalar.copy, v_bf_first[:, n], v_raw_first[:, n])
 
         size_pairs = size_ps[:].rearrange("q (u r) s -> q u s r", u=2)
         sized = [sb.tile([P, 2, P // 2, 2], F32, name="sized%d" % h, align_bytes=MX_ALIGN) for h in range(2)]
         nc.vector.tensor_tensor(sized[0][:], probs[0], size_pairs[:, :, 0 : P // 2, :], ALU.mult)
         row_sum = sb.tile([P, 1], F32, name="row_sum")
         nc.vector.tensor_scalar(row_sum[:], first_sum_less_one[:], shift, sums[1][:], ALU.mult, ALU.add)
-        nc.vector.tensor_tensor(sized[1][:], probs[1], size_pairs[:, :, P // 2 : P, :], ALU.mult)
+        nc.vector.tensor_tensor(sized[1][:, 0], probs[1][:, 0], size_pairs[:, 0, P // 2 : P, :], ALU.mult)
         inv_sum = sb.tile([P, 1], F32, name="inv_sum")
         nc.vector.reciprocal(inv_sum[:], row_sum[:])
+        nc.vector.tensor_tensor(sized[1][:, 1], probs[1][:, 1], size_pairs[:, 1, P // 2 : P, :], ALU.mult)
         turned = ps.tile([P, 2, Q], F32, name="turned", tag="bank1")
         for u in range(2):
             w_pair = sb.tile([P, P, 2], BF16, name="w_pair%d" % u)
@@ -163,7 +166,8 @@ def tile_attend_pqkeys_kernel(tc, book_words, book_scales, query, size, vals, of
         v_words_first = sb.tile([P, HALF], U32, name="v_words_first", tag="sized0", align_bytes=MX_ALIGN)
         v_words = [v_words_first[:, 0:QUARTER], v_words_first[:, QUARTER:HALF]]
         quantise_values(v_words[0], v_planes[0][:], v_bf_first[:, 0])
-        interleave(nc.vector.tensor_copy, v_bf_second[:], v_raw_second[:])
+        for n in range(2):
+            interleave(nc.vector.tensor_copy, v_bf_second[:, n * QUARTER : (n + 1) * QUARTER], v_raw_second[:, n])
         quantise_values(v_words[1], v_planes[1][:], v_bf_first[:, 1])
 
         w_words = sb.tile([P, Q], U32, name="w_words", align_bytes=MX_ALIGN)

@@ -63,9 +63,9 @@ def tile_attend_pqkeys_kernel(tc, book_words, book_scales, query, size, vals, of
         ident = sb.tile([P, P], F32, name="ident")
         nc.scalar.activation(ident[:], off_diagonal[:], ACT.Copy, bias=1.0, scale=-1.0)
 
-        size_ps = ps.tile([P, PACK, P], F32, name="size_ps")
+        size_ps = ps.tile([P, 2, P, 2], F32, name="size_ps")
         for t in range(PACK):
-            nc.tensor.transpose(size_ps[:, t, :], size_col[:, t : t + 1].to_broadcast([P, P]), ident[:])
+            nc.tensor.transpose(size_ps[:, t // 2, :, t % 2], size_col[:, t : t + 1].to_broadcast([P, P]), ident[:])
 
         def interleave(copy, dst, src):
             copy(dst.rearrange("p (c n) t -> p c t n", n=4), src.rearrange("p t (c n) -> p c t n", n=4))
@@ -142,10 +142,10 @@ def tile_attend_pqkeys_kernel(tc, book_words, book_scales, query, size, vals, of
         for n in range(2):
             interleave(nc.scalar.copy, v_bf_first[:, n], v_raw_first[:, n])
 
-        size_pairs = size_ps[:].rearrange("q (u r) s -> q u s r", u=2)
+        size_pairs = size_ps[:]
         sized = [sb.tile([P, 2, P // 2, 2], F32, name="sized%d" % h, align_bytes=MX_ALIGN) for h in range(2)]
         nc.vector.tensor_tensor(sized[0][:], probs[0], size_pairs[:, :, 0 : P // 2, :], ALU.mult)
-        row_sum = sb.tile([P, 1], F32, name="row_sum")
+        row_sum = sb.tile([P, 1], F32, name="row_sum", align_bytes=MX_ALIGN)
         nc.vector.tensor_scalar(row_sum[:], first_sum_less_one[:], shift, sums[1][:], ALU.mult, ALU.add)
         nc.vector.tensor_tensor(sized[1][:, 0], probs[1][:, 0], size_pairs[:, 0, P // 2 : P, :], ALU.mult)
         inv_sum = sb.tile([P, 1], F32, name="inv_sum")
@@ -163,7 +163,7 @@ def tile_attend_pqkeys_kernel(tc, book_words, book_scales, query, size, vals, of
             )
 
         v_bf_second = sb.tile([P, HALF, PACK], BF16, name="v_bf_second", tag="sized1", align_bytes=MX_ALIGN)
-        v_words_first = sb.tile([P, HALF], U32, name="v_words_first", tag="sized0", align_bytes=MX_ALIGN)
+        v_words_first = sb.tile([P, HALF], U32, name="v_words_first", tag="row_sum", align_bytes=MX_ALIGN)
         v_words = [v_words_first[:, 0:QUARTER], v_words_first[:, QUARTER:HALF]]
         quantise_values(v_words[0], v_planes[0][:], v_bf_first[:, 0])
         for n in range(2):

@@ -23,6 +23,7 @@ SLOTS = I // 2
 HALF = E // 2
 QUARTER = E // 4
 MX_ALIGN = 64
+FACTOR_CAP = 2.0**58
 FLOPS = 2 * Q * I * D + 2 * Q * E * I
 
 
@@ -117,25 +118,20 @@ def tile_attend_pqkeys_kernel(tc, book_words, book_scales, query, size, vals, of
                 rhs=key_words[h][:].bitcast(FP8X4), rhs_scale=key_planes[h][:], start=True, stop=True,
             )
             scores.append(bank[:])
-        def paired(cols):
-            return cols.rearrange("q (u s r) -> q u s r", u=2, r=2)
-
-        probs_first = sb.tile([P, SLOTS], F32, name="probs_first", align_bytes=MX_ALIGN)
-        probs_second = sb.tile([P, SLOTS + 1], F32, name="probs_second", align_bytes=MX_ALIGN)
-        probs = [paired(probs_first[:]), paired(probs_second[:, 0:SLOTS])]
-        shift = probs_second[:, SLOTS : SLOTS + 1]
+        probs = [sb.tile([P, 2, P // 2, 2], F32, name="probs%d" % h, align_bytes=MX_ALIGN)[:] for h in range(2)]
         sums = [sb.tile([P, 1], F32, name="sum%d" % h) for h in range(2)]
-        negated = sb.tile([P, SLOTS + 1], F32, name="negated", tag="scores_then_values", align_bytes=MX_ALIGN)
-        neg_first_max = negated[:, SLOTS : SLOTS + 1]
-        nc.vector.tensor_reduce(neg_first_max, scores[0], AXIS.X, ALU.max, negate=True)
-        nc.scalar.activation(probs[0], by_pairs(scores[0]), ACT.Exp, bias=neg_first_max, accum_out=sums[0][:])
-        neg_max = sb.tile([P, 1], F32, name="neg_max")
-        nc.vector.tensor_scalar(
-            paired(negated[:, 0:SLOTS]), by_pairs(scores[1]), -1.0, neg_first_max, ALU.mult, ALU.min, accum_out=neg_max[:]
-        )
-        nc.scalar.activation(probs_second[:], negated[:], ACT.Exp, bias=neg_max[:], scale=-1.0, accum_out=sums[1][:])
-        first_sum_less_one = sb.tile([P, 1], F32, name="first_sum_less_one")
-        nc.vector.tensor_scalar(first_sum_less_one[:], sums[0][:], -1.0, None, ALU.add)
+        neg_max = [
+            sb.tile([P, 1], F32, name="neg_max0"),
+            sb.tile([P, 1], F32, name="neg_max1", tag="scores_then_values", align_bytes=MX_ALIGN),
+        ]
+        for h in range(2):
+            nc.vector.tensor_reduce(neg_max[h][:], scores[h], AXIS.X, ALU.max, negate=True)
+        nc.scalar.activation(probs[0], by_pairs(scores[0]), ACT.Exp, bias=neg_max[0][:], accum_out=sums[0][:])
+        ratio = sb.tile([P, 1], F32, name="ratio")
+        nc.scalar.activation(ratio[:], neg_max[0][:], ACT.Exp, bias=neg_max[1][:], scale=-1.0)
+        nc.scalar.activation(probs[1], by_pairs(scores[1]), ACT.Exp, bias=neg_max[1][:], accum_out=sums[1][:])
+        factor = sb.tile([P, 1], F32, name="factor")
+        nc.vector.tensor_scalar(factor[:], ratio[:], FACTOR_CAP, None, ALU.min)
 
         v_planes = [sb.tile([P, QUARTER], U8, name="v_plane%d" % n, align_bytes=MX_ALIGN) for n in range(4)]
         v_bf_first = sb.tile([P, 2, QUARTER, PACK], BF16, name="v_bf_first", tag="scores_then_values", align_bytes=MX_ALIGN)
@@ -146,16 +142,16 @@ def tile_attend_pqkeys_kernel(tc, book_words, book_scales, query, size, vals, of
         sized = [sb.tile([P, 2, P // 2, 2], F32, name="sized%d" % h, align_bytes=MX_ALIGN) for h in range(2)]
         nc.vector.tensor_tensor(sized[0][:], probs[0], size_pairs[:, :, 0 : P // 2, :], ALU.mult)
         row_sum = sb.tile([P, 1], F32, name="row_sum", align_bytes=MX_ALIGN)
-        nc.vector.tensor_scalar(row_sum[:], first_sum_less_one[:], shift, sums[1][:], ALU.mult, ALU.add)
+        nc.vector.tensor_scalar(row_sum[:], sums[0][:], factor[:], sums[1][:], ALU.mult, ALU.add)
         nc.vector.tensor_tensor(sized[1][:, 0], probs[1][:, 0], size_pairs[:, 0, P // 2 : P, :], ALU.mult)
         inv_sum = sb.tile([P, 1], F32, name="inv_sum")
         nc.vector.reciprocal(inv_sum[:], row_sum[:])
         nc.vector.tensor_tensor(sized[1][:, 1], probs[1][:, 1], size_pairs[:, 1, P // 2 : P, :], ALU.mult)
-        turned = ps.tile([P, 2, Q], F32, name="turned", tag="bank1")
+        turned = ps.tile([P, 2, Q], F32, name="turned", tag="bank0")
         for u in range(2):
             w_pair = sb.tile([P, P, 2], BF16, name="w_pair%d" % u)
             nc.vector.tensor_scalar(
-                w_pair[:, 0 : P // 2, :], sized[0][:, u], shift, inv_sum[:], ALU.mult, ALU.mult
+                w_pair[:, 0 : P // 2, :], sized[0][:, u], factor[:], inv_sum[:], ALU.mult, ALU.mult
             )
             nc.vector.tensor_scalar(w_pair[:, P // 2 : P, :], sized[1][:, u], inv_sum[:], None, ALU.mult)
             nc.tensor.transpose(

@@ -23,7 +23,7 @@ SLOTS = I // 2
 HALF = E // 2
 QUARTER = E // 4
 MX_ALIGN = 64
-FACTOR_CAP = 2.0**58
+LEAD_CAP = 40.0
 FLOPS = 2 * Q * I * D + 2 * Q * E * I
 
 
@@ -127,11 +127,11 @@ def tile_attend_pqkeys_kernel(tc, book_words, book_scales, query, size, vals, of
         for h in range(2):
             nc.vector.tensor_reduce(neg_max[h][:], scores[h], AXIS.X, ALU.max, negate=True)
         nc.scalar.activation(probs[0], by_pairs(scores[0]), ACT.Exp, bias=neg_max[0][:], accum_out=sums[0][:])
-        ratio = sb.tile([P, 1], F32, name="ratio")
-        nc.scalar.activation(ratio[:], neg_max[0][:], ACT.Exp, bias=neg_max[1][:], scale=-1.0)
         nc.scalar.activation(probs[1], by_pairs(scores[1]), ACT.Exp, bias=neg_max[1][:], accum_out=sums[1][:])
+        lead = sb.tile([P, 1], F32, name="lead")
+        nc.vector.tensor_scalar(lead[:], neg_max[1][:], neg_max[0][:], LEAD_CAP, ALU.subtract, ALU.min)
         factor = sb.tile([P, 1], F32, name="factor")
-        nc.vector.tensor_scalar(factor[:], ratio[:], FACTOR_CAP, None, ALU.min)
+        nc.scalar.activation(factor[:], lead[:], ACT.Exp)
 
         v_planes = [sb.tile([P, QUARTER], U8, name="v_plane%d" % n, align_bytes=MX_ALIGN) for n in range(4)]
         v_bf_first = sb.tile([P, 2, QUARTER, PACK], BF16, name="v_bf_first", tag="scores_then_values", align_bytes=MX_ALIGN)

@@ -98,11 +98,10 @@ def tile_attend_pqkeys_kernel(tc, book_words, book_scales, query, size, vals, of
         q_plane = sb.tile([P, Q], U8, name="q_plane", align_bytes=MX_ALIGN)
         nc.vector.quantize_mx(q_words[:].bitcast(FP8X4), q_plane[:], q_bf[:].rearrange("p q t -> p (q t)"))
 
-        key_words = []
+        got_words = sb.tile([P, I], U32, name="got_words", tag="q_bf", align_bytes=MX_ALIGN)
+        key_words = [got_words[:, h * SLOTS : (h + 1) * SLOTS] for h in range(2)]
         for h in range(2):
-            words = sb.tile([P, SLOTS], U32, name="key_words%d" % h, align_bytes=MX_ALIGN)
-            nc.vector.tensor_copy(words[:], word_win[:].bitcast(U32).indirect(offsets[:, halves[h]]))
-            key_words.append(words)
+            nc.vector.tensor_copy(key_words[h], word_win[:].bitcast(U32).indirect(offsets[:, halves[h]]))
         v_raw_second = sb.tile([P, 2, PACK, QUARTER], F32, name="v_raw_second", tag="queries_then_values")
         for n in range(2):
             nc.scalar.dma_start(out=v_raw_second[:, n], in_=v_rows[:, :, HALF + n * QUARTER : HALF + (n + 1) * QUARTER])
@@ -115,7 +114,7 @@ def tile_attend_pqkeys_kernel(tc, book_words, book_scales, query, size, vals, of
             bank = ps.tile([P, SLOTS], F32, name="scores%d" % h, tag="bank%d" % h)
             nc.tensor.matmul_mx(
                 bank[:], lhsT=q_words[:].bitcast(FP8X4), lhsT_scale=q_plane[:],
-                rhs=key_words[h][:].bitcast(FP8X4), rhs_scale=key_planes[h][:], start=True, stop=True,
+                rhs=key_words[h].bitcast(FP8X4), rhs_scale=key_planes[h][:], start=True, stop=True,
             )
             scores.append(bank[:])
         probs = [sb.tile([P, 2, P // 2, 2], F32, name="probs%d" % h, align_bytes=MX_ALIGN)[:] for h in range(2)]

@@ -44,7 +44,7 @@ def tile_attend_pqkeys_kernel(tc, book_words, book_scales, query, size, vals, of
         size_col = sb.tile([P, PACK], F32, name="size_col")
         nc.sync.dma_start(out=size_col[:], in_=size.rearrange("o (p t) -> (o p) t", t=PACK))
 
-        q_raw = sb.tile([P, PACK, Q], F32, name="q_raw", tag="queries_then_values")
+        q_raw = sb.tile([P, PACK, Q], F32, name="q_raw", tag="queries_then_words", align_bytes=MX_ALIGN)
         nc.scalar.dma_start(out=q_raw[:], in_=query.rearrange("(p t) q -> p t q", t=PACK))
         word_win = sb.tile([P, C], I32, name="word_win", align_bytes=MX_ALIGN)
         nc.scalar.dma_start(out=word_win[:], in_=book_words[0].rearrange("p c r -> p (c r)").bitcast(I32))
@@ -98,11 +98,11 @@ def tile_attend_pqkeys_kernel(tc, book_words, book_scales, query, size, vals, of
         q_plane = sb.tile([P, Q], U8, name="q_plane", align_bytes=MX_ALIGN)
         nc.vector.quantize_mx(q_words[:].bitcast(FP8X4), q_plane[:], q_bf[:].rearrange("p q t -> p (q t)"))
 
-        got_words = sb.tile([P, I], U32, name="got_words", tag="q_bf", align_bytes=MX_ALIGN)
+        got_words = sb.tile([P, I], U32, name="got_words", tag="queries_then_words", align_bytes=MX_ALIGN)
         key_words = [got_words[:, h * SLOTS : (h + 1) * SLOTS] for h in range(2)]
         for h in range(2):
             nc.vector.tensor_copy(key_words[h], word_win[:].bitcast(U32).indirect(offsets[:, halves[h]]))
-        v_raw_second = sb.tile([P, 2, PACK, QUARTER], F32, name="v_raw_second", tag="queries_then_values")
+        v_raw_second = sb.tile([P, 2, PACK, QUARTER], F32, name="v_raw_second", tag="q_bf", align_bytes=MX_ALIGN)
         for n in range(2):
             nc.scalar.dma_start(out=v_raw_second[:, n], in_=v_rows[:, :, HALF + n * QUARTER : HALF + (n + 1) * QUARTER])
 
@@ -161,9 +161,9 @@ def tile_attend_pqkeys_kernel(tc, book_words, book_scales, query, size, vals, of
         v_words_first = sb.tile([P, HALF], U32, name="v_words_first", tag="row_sum", align_bytes=MX_ALIGN)
         v_words = [v_words_first[:, 0:QUARTER], v_words_first[:, QUARTER:HALF]]
         quantise_values(v_words[0], v_planes[0][:], v_bf_first[:, 0])
-        for n in range(2):
-            interleave(nc.vector.tensor_copy, v_bf_second[:, n * QUARTER : (n + 1) * QUARTER], v_raw_second[:, n])
+        interleave(nc.vector.tensor_copy, v_bf_second[:, 0:QUARTER], v_raw_second[:, 0])
         quantise_values(v_words[1], v_planes[1][:], v_bf_first[:, 1])
+        interleave(nc.vector.tensor_copy, v_bf_second[:, QUARTER:HALF], v_raw_second[:, 1])
 
         w_words = sb.tile([P, Q], U32, name="w_words", align_bytes=MX_ALIGN)
         w_plane = sb.tile([P, Q], U8, name="w_plane", align_bytes=MX_ALIGN)

@@ -118,7 +118,7 @@ def tile_attend_pqkeys_kernel(tc, book_words, book_scales, query, size, vals, of
             )
             scores.append(bank[:])
         probs = [sb.tile([P, 2, P // 2, 2], F32, name="probs%d" % h, align_bytes=MX_ALIGN)[:] for h in range(2)]
-        sums = [sb.tile([P, 1], F32, name="sum%d" % h) for h in range(2)]
+        sums = [sb.tile([P, 1], F32, name="sum%d" % h, align_bytes=MX_ALIGN) for h in range(2)]
         neg_max = [
             sb.tile([P, 1], F32, name="neg_max0"),
             sb.tile([P, 1], F32, name="neg_max1", tag="scores_then_values", align_bytes=MX_ALIGN),
@@ -127,7 +127,7 @@ def tile_attend_pqkeys_kernel(tc, book_words, book_scales, query, size, vals, of
             nc.vector.tensor_reduce(neg_max[h][:], scores[h], AXIS.X, ALU.max, negate=True)
         nc.scalar.activation(probs[0], by_pairs(scores[0]), ACT.Exp, bias=neg_max[0][:], accum_out=sums[0][:])
         nc.scalar.activation(probs[1], by_pairs(scores[1]), ACT.Exp, bias=neg_max[1][:], accum_out=sums[1][:])
-        lead = sb.tile([P, 1], F32, name="lead")
+        lead = sb.tile([P, 1], F32, name="lead", align_bytes=MX_ALIGN)
         nc.vector.tensor_scalar(lead[:], neg_max[1][:], neg_max[0][:], LEAD_CAP, ALU.subtract, ALU.min)
         factor = sb.tile([P, 1], F32, name="factor")
         nc.scalar.activation(factor[:], lead[:], ACT.Exp)
@@ -138,26 +138,30 @@ def tile_attend_pqkeys_kernel(tc, book_words, book_scales, query, size, vals, of
             interleave(nc.scalar.copy, v_bf_first[:, n], v_raw_first[:, n])
 
         size_pairs = size_ps[:]
-        sized = [sb.tile([P, 2, P // 2, 2], F32, name="sized%d" % h, align_bytes=MX_ALIGN) for h in range(2)]
-        nc.vector.tensor_tensor(sized[0][:], probs[0], size_pairs[:, :, 0 : P // 2, :], ALU.mult)
+        sized_first = sb.tile([P, 2, P // 2, 2], F32, name="sized_first", align_bytes=MX_ALIGN)
+        sized_second = [
+            sb.tile([P, P // 2, 2], F32, name="sized_second%d" % u, tag=("lead", "sum0")[u], align_bytes=MX_ALIGN)
+            for u in range(2)
+        ]
+        nc.vector.tensor_tensor(sized_first[:], probs[0], size_pairs[:, :, 0 : P // 2, :], ALU.mult)
         row_sum = sb.tile([P, 1], F32, name="row_sum", align_bytes=MX_ALIGN)
         nc.vector.tensor_scalar(row_sum[:], sums[0][:], factor[:], sums[1][:], ALU.mult, ALU.add)
-        nc.vector.tensor_tensor(sized[1][:, 0], probs[1][:, 0], size_pairs[:, 0, P // 2 : P, :], ALU.mult)
+        nc.vector.tensor_tensor(sized_second[0][:], probs[1][:, 0], size_pairs[:, 0, P // 2 : P, :], ALU.mult)
         inv_sum = sb.tile([P, 1], F32, name="inv_sum")
         nc.vector.reciprocal(inv_sum[:], row_sum[:])
-        nc.vector.tensor_tensor(sized[1][:, 1], probs[1][:, 1], size_pairs[:, 1, P // 2 : P, :], ALU.mult)
+        nc.vector.tensor_tensor(sized_second[1][:], probs[1][:, 1], size_pairs[:, 1, P // 2 : P, :], ALU.mult)
         turned = ps.tile([P, 2, Q], F32, name="turned", tag="bank0")
         for u in range(2):
             w_pair = sb.tile([P, P, 2], BF16, name="w_pair%d" % u)
             nc.vector.tensor_scalar(
-                w_pair[:, 0 : P // 2, :], sized[0][:, u], factor[:], inv_sum[:], ALU.mult, ALU.mult
+                w_pair[:, 0 : P // 2, :], sized_first[:, u], factor[:], inv_sum[:], ALU.mult, ALU.mult
             )
-            nc.vector.tensor_scalar(w_pair[:, P // 2 : P, :], sized[1][:, u], inv_sum[:], None, ALU.mult)
+            nc.vector.tensor_scalar(w_pair[:, P // 2 : P, :], sized_second[u][:], inv_sum[:], None, ALU.mult)
             nc.tensor.transpose(
                 turned[:, u, :], w_pair[:].rearrange("q s r -> q (s r)").bitcast(F32), ident[:]
             )
 
-        v_bf_second = sb.tile([P, HALF, PACK], BF16, name="v_bf_second", tag="sized1", align_bytes=MX_ALIGN)
+        v_bf_second = sb.tile([P, HALF, PACK], BF16, name="v_bf_second", tag="sum0", align_bytes=MX_ALIGN)
         v_words_first = sb.tile([P, HALF], U32, name="v_words_first", tag="row_sum", align_bytes=MX_ALIGN)
         v_words = [v_words_first[:, 0:QUARTER], v_words_first[:, QUARTER:HALF]]
         quantise_values(v_words[0], v_planes[0][:], v_bf_first[:, 0])
@@ -170,8 +174,8 @@ def tile_attend_pqkeys_kernel(tc, book_words, book_scales, query, size, vals, of
         for rows in (slice(0, Q // 2), slice(Q // 2, Q)):
             wt_bf = sb.tile([P, Q // 2 * PACK], BF16, name="wt_bf%d" % rows.start, align_bytes=MX_ALIGN)
             nc.scalar.copy(
-                wt_bf[:].bitcast(F32).rearrange("s (q u) -> s q u", u=2),
-                turned[:, :, rows].rearrange("s u q -> s q u"),
+                wt_bf[:].bitcast(F32).rearrange("s (c n u) -> s c u n", n=2, u=2),
+                turned[:, :, rows].rearrange("s u (c n) -> s c u n", n=2),
             )
             nc.vector.quantize_mx(w_words[:, rows].bitcast(FP8X4), w_plane[:, rows], wt_bf[:])
         for n, src in ((2, v_bf_second[:, 0:QUARTER]), (3, v_bf_second[:, QUARTER:HALF])):

@@ -75,10 +75,9 @@ def tile_attend_pqkeys_kernel(tc, book_words, book_scales, query, size, vals, of
             nc.vector.quantize_mx(words.bitcast(FP8X4), plane, src.rearrange("p e t -> p (e t)"))
 
         q_bf = sb.tile([P, Q, PACK], BF16, name="q_bf", align_bytes=MX_ALIGN)
-        interleave(nc.scalar.copy, q_bf[:], q_raw[:])
 
         halves = [slice(h * SLOTS // GROUP, (h + 1) * SLOTS // GROUP) for h in range(2)]
-        move_queues = ((nc.sync, nc.sync, nc.scalar, nc.sync), (nc.sync, nc.scalar, nc.sync, nc.scalar))
+        move_queues = ((nc.sync, nc.scalar, nc.sync, nc.scalar),) * 2
         key_planes = []
         for h in range(2):
             key_plane = sb.tile([P, SLOTS], U8, name="key_plane%d" % h, align_bytes=MX_ALIGN)
@@ -96,7 +95,11 @@ def tile_attend_pqkeys_kernel(tc, book_words, book_scales, query, size, vals, of
             nc.scalar.dma_start(out=v_raw_first[:, n], in_=v_rows[:, :, n * QUARTER : (n + 1) * QUARTER])
         q_words = sb.tile([P, Q], U32, name="q_words", align_bytes=MX_ALIGN)
         q_plane = sb.tile([P, Q], U8, name="q_plane", align_bytes=MX_ALIGN)
-        nc.vector.quantize_mx(q_words[:].bitcast(FP8X4), q_plane[:], q_bf[:].rearrange("p q t -> p (q t)"))
+        q_halves = (slice(0, Q // 2), slice(Q // 2, Q))
+        for rows in q_halves:
+            interleave(nc.vector.tensor_copy, q_bf[:, rows], q_raw[:, :, rows])
+        for rows in q_halves:
+            quantise_values(q_words[:, rows], q_plane[:, rows], q_bf[:, rows])
 
         got_words = sb.tile([P, I], U32, name="got_words", tag="queries_then_words", align_bytes=MX_ALIGN)
         key_words = [got_words[:, h * SLOTS : (h + 1) * SLOTS] for h in range(2)]

from contextlib import ExitStack

import concourse.mybir as mybir

F32 = mybir.dt.float32
BF16 = mybir.dt.bfloat16
I32 = mybir.dt.int32
U32 = mybir.dt.uint32
U16 = mybir.dt.uint16
U8 = mybir.dt.uint8
FP8X4 = mybir.dt.float8_e4m3fn_x4
ALU = mybir.AluOpType
ACT = mybir.ActivationFunctionType
AXIS = mybir.AxisListType

P = 128
PACK = 4
BLOCK_ROWS = 8
QUADRANT = 32
GROUP = 16
D, C, I, Q, E = 512, 1024, 512, 128, 512
SLOTS = I // 2
HALF = E // 2
QUARTER = E // 4
MX_ALIGN = 64
LEAD_CAP = 40.0
FLOPS = 2 * Q * I * D + 2 * Q * E * I


def tile_attend_pqkeys_kernel(tc, book_words, book_scales, query, size, vals, offs, out):
    nc = tc.nc
    with ExitStack() as ctx:
        sb = ctx.enter_context(tc.tile_pool(name="sb", bufs=1))
        ps = ctx.enter_context(tc.psum_pool(name="ps", bufs=1))

        scale_win = sb.tile([P, C], U8, name="scale_win", tag="scales_values_sum", align_bytes=MX_ALIGN)
        nc.scalar.dma_start(
            out=scale_win[:].bitcast(I32),
            in_=book_scales[0].bitcast(I32).unsqueeze(1).to_broadcast([P // BLOCK_ROWS, BLOCK_ROWS, C // 4]),
        )
        offsets = sb.tile([P, I // GROUP], U16, name="offsets")
        nc.sync.dma_start(offsets[:], offs)
        v_rows = vals.rearrange("(p t) e -> p t e", t=PACK)
        size_col = sb.tile([P, PACK], F32, name="size_col")
        nc.sync.dma_start(out=size_col[:], in_=size.rearrange("o (p t) -> (o p) t", t=PACK))

        q_raw = sb.tile([P, PACK, Q], F32, name="q_raw", tag="queries_then_words", align_bytes=MX_ALIGN)
        nc.scalar.dma_start(out=q_raw[:], in_=query.rearrange("(p t) q -> p t q", t=PACK))
        word_win = sb.tile([P, C], I32, name="word_win", align_bytes=MX_ALIGN)
        nc.scalar.dma_start(out=word_win[:], in_=book_words[0].rearrange("p c r -> p (c r)").bitcast(I32))

        one = sb.tile([P, 1], F32, name="one")
        nc.vector.memset(one[:], 1.0)
        base = sb.tile([P, 1], F32, name="base")
        for first in range(0, P, QUADRANT):
            nc.gpsimd.memset(base[first : first + QUADRANT, :], float(first))
        col = sb.tile([P, P], F32, name="col", align_bytes=MX_ALIGN)
        ones = one[:].to_broadcast([P, P])
        nc.vector.tensor_tensor_scan(col[:], ones, ones, 0.0, ALU.mult, ALU.add)
        row = sb.tile([P, QUADRANT], F32, name="row", align_bytes=MX_ALIGN)
        nc.vector.transpose(row[:], col[:, 0:QUADRANT])
        off_diagonal = sb.tile([P, P], F32, name="off_diagonal")
        nc.vector.tensor_scalar(off_diagonal[:], col[:], base[:], row[:, 0:1], ALU.subtract, ALU.not_equal)
        ident = sb.tile([P, P], F32, name="ident")
        nc.scalar.activation(ident[:], off_diagonal[:], ACT.Copy, bias=1.0, scale=-1.0)

        size_ps = ps.tile([P, 2, P, 2], F32, name="size_ps")
        for t in range(PACK):
            nc.tensor.transpose(size_ps[:, t // 2, :, t % 2], size_col[:, t : t + 1].to_broadcast([P, P]), ident[:])

        def interleave(copy, dst, src):
            copy(dst.rearrange("p (c n) t -> p c t n", n=4), src.rearrange("p t (c n) -> p c t n", n=4))

        def quantise_values(words, plane, src):
            nc.vector.quantize_mx(words.bitcast(FP8X4), plane, src.rearrange("p e t -> p (e t)"))

        q_bf = sb.tile([P, Q, PACK], BF16, name="q_bf", align_bytes=MX_ALIGN)

        halves = [slice(h * SLOTS // GROUP, (h + 1) * SLOTS // GROUP) for h in range(2)]
        move_queues = ((nc.sync, nc.scalar, nc.sync, nc.scalar),) * 2
        key_planes = []
        for h in range(2):
            key_plane = sb.tile([P, SLOTS], U8, name="key_plane%d" % h, align_bytes=MX_ALIGN)
            nc.vector.memset(key_plane[:].bitcast(I32), 0)
            got_scales = sb.tile([P, SLOTS], U8, name="got_scales%d" % h, align_bytes=MX_ALIGN)
            nc.vector.tensor_copy(got_scales[:], scale_win[:].indirect(offsets[:, halves[h]]))
            for j in range(QUADRANT // BLOCK_ROWS):
                move_queues[h][j].dma_start(
                    out=key_plane[:].bitcast(I32)[j:P:QUADRANT, :],
                    in_=got_scales[:].bitcast(I32)[BLOCK_ROWS * j : P : QUADRANT, :],
                )
            key_planes.append(key_plane)
        v_raw_first = sb.tile([P, 2, PACK, QUARTER], F32, name="v_raw_first", tag="scales_values_sum", align_bytes=MX_ALIGN)
        for n in range(2):
            nc.scalar.dma_start(out=v_raw_first[:, n], in_=v_rows[:, :, n * QUARTER : (n + 1) * QUARTER])
        q_words = sb.tile([P, Q], U32, name="q_words", align_bytes=MX_ALIGN)
        q_plane = sb.tile([P, Q], U8, name="q_plane", align_bytes=MX_ALIGN)
        q_halves = (slice(0, Q // 2), slice(Q // 2, Q))
        for rows in q_halves:
            interleave(nc.vector.tensor_copy, q_bf[:, rows], q_raw[:, :, rows])
        for rows in q_halves:
            quantise_values(q_words[:, rows], q_plane[:, rows], q_bf[:, rows])

        got_words = sb.tile([P, I], U32, name="got_words", tag="queries_then_words", align_bytes=MX_ALIGN)
        key_words = [got_words[:, h * SLOTS : (h + 1) * SLOTS] for h in range(2)]
        for h in range(2):
            nc.vector.tensor_copy(key_words[h], word_win[:].bitcast(U32).indirect(offsets[:, halves[h]]))
        v_raw_second = sb.tile([P, 2, PACK, QUARTER], F32, name="v_raw_second", tag="q_bf", align_bytes=MX_ALIGN)
        for n in range(2):
            nc.scalar.dma_start(out=v_raw_second[:, n], in_=v_rows[:, :, HALF + n * QUARTER : HALF + (n + 1) * QUARTER])

        def by_pairs(row):
            return row.rearrange("q (s u r) -> q u s r", u=2, r=2)

        scores = []
        for h in range(2):
            bank = ps.tile([P, SLOTS], F32, name="scores%d" % h, tag="bank%d" % h)
            nc.tensor.matmul_mx(
                bank[:], lhsT=q_words[:].bitcast(FP8X4), lhsT_scale=q_plane[:],
                rhs=key_words[h].bitcast(FP8X4), rhs_scale=key_planes[h][:], start=True, stop=True,
            )
            scores.append(bank[:])
        probs = [sb.tile([P, 2, P // 2, 2], F32, name="probs%d" % h, align_bytes=MX_ALIGN)[:] for h in range(2)]
        sums = [sb.tile([P, 1], F32, name="sum%d" % h, align_bytes=MX_ALIGN) for h in range(2)]
        neg_max = [
            sb.tile([P, 1], F32, name="neg_max0"),
            sb.tile([P, 1], F32, name="neg_max1", tag="scores_then_values", align_bytes=MX_ALIGN),
        ]
        for h in range(2):
            nc.vector.tensor_reduce(neg_max[h][:], scores[h], AXIS.X, ALU.max, negate=True)
        nc.scalar.activation(probs[0], by_pairs(scores[0]), ACT.Exp, bias=neg_max[0][:], accum_out=sums[0][:])
        nc.scalar.activation(probs[1], by_pairs(scores[1]), ACT.Exp, bias=neg_max[1][:], accum_out=sums[1][:])
        lead = sb.tile([P, 1], F32, name="lead", align_bytes=MX_ALIGN)
        nc.vector.tensor_scalar(lead[:], neg_max[1][:], neg_max[0][:], LEAD_CAP, ALU.subtract, ALU.min)
        factor = sb.tile([P, 1], F32, name="factor")
        nc.scalar.activation(factor[:], lead[:], ACT.Exp)

        v_planes = [sb.tile([P, QUARTER], U8, name="v_plane%d" % n, align_bytes=MX_ALIGN) for n in range(4)]
        v_bf_first = sb.tile([P, 2, QUARTER, PACK], BF16, name="v_bf_first", tag="scores_then_values", align_bytes=MX_ALIGN)
        for n in range(2):
            interleave(nc.scalar.copy, v_bf_first[:, n], v_raw_first[:, n])

        size_pairs = size_ps[:]
        sized_first = sb.tile([P, 2, P // 2, 2], F32, name="sized_first", align_bytes=MX_ALIGN)
        sized_second = [
            sb.tile([P, P // 2, 2], F32, name="sized_second%d" % u, tag=("lead", "sum0")[u], align_bytes=MX_ALIGN)
            for u in range(2)
        ]
        nc.vector.tensor_tensor(sized_first[:], probs[0], size_pairs[:, :, 0 : P // 2, :], ALU.mult)
        row_sum = sb.tile([P, 1], F32, name="row_sum", align_bytes=MX_ALIGN)
        nc.vector.tensor_scalar(row_sum[:], sums[0][:], factor[:], sums[1][:], ALU.mult, ALU.add)
        nc.vector.tensor_tensor(sized_second[0][:], probs[1][:, 0], size_pairs[:, 0, P // 2 : P, :], ALU.mult)
        inv_sum = sb.tile([P, 1], F32, name="inv_sum")
        nc.vector.reciprocal(inv_sum[:], row_sum[:])
        nc.vector.tensor_tensor(sized_second[1][:], probs[1][:, 1], size_pairs[:, 1, P // 2 : P, :], ALU.mult)
        turned = ps.tile([P, 2, Q], F32, name="turned", tag="bank0")
        for u in range(2):
            w_pair = sb.tile([P, P, 2], BF16, name="w_pair%d" % u)
            nc.vector.tensor_scalar(
                w_pair[:, 0 : P // 2, :], sized_first[:, u], factor[:], inv_sum[:], ALU.mult, ALU.mult
            )
            nc.vector.tensor_scalar(w_pair[:, P // 2 : P, :], sized_second[u][:], inv_sum[:], None, ALU.mult)
            nc.tensor.transpose(
                turned[:, u, :], w_pair[:].rearrange("q s r -> q (s r)").bitcast(F32), ident[:]
            )

        v_bf_second = sb.tile([P, HALF, PACK], BF16, name="v_bf_second", tag="sum0", align_bytes=MX_ALIGN)
        v_words_first = sb.tile([P, HALF], U32, name="v_words_first", tag="row_sum", align_bytes=MX_ALIGN)
        v_words = [v_words_first[:, 0:QUARTER], v_words_first[:, QUARTER:HALF]]
        quantise_values(v_words[0], v_planes[0][:], v_bf_first[:, 0])
        interleave(nc.vector.tensor_copy, v_bf_second[:, 0:QUARTER], v_raw_second[:, 0])
        quantise_values(v_words[1], v_planes[1][:], v_bf_first[:, 1])
        interleave(nc.vector.tensor_copy, v_bf_second[:, QUARTER:HALF], v_raw_second[:, 1])

        w_words = sb.tile([P, Q], U32, name="w_words", align_bytes=MX_ALIGN)
        w_plane = sb.tile([P, Q], U8, name="w_plane", align_bytes=MX_ALIGN)
        for rows in (slice(0, Q // 2), slice(Q // 2, Q)):
            wt_bf = sb.tile([P, Q // 2 * PACK], BF16, name="wt_bf%d" % rows.start, align_bytes=MX_ALIGN)
            nc.scalar.copy(
                wt_bf[:].bitcast(F32).rearrange("s (c n u) -> s c u n", n=2, u=2),
                turned[:, :, rows].rearrange("s u (c n) -> s c u n", n=2),
            )
            nc.vector.quantize_mx(w_words[:, rows].bitcast(FP8X4), w_plane[:, rows], wt_bf[:])
        for n, src in ((2, v_bf_second[:, 0:QUARTER]), (3, v_bf_second[:, QUARTER:HALF])):
            words = sb.tile([P, QUARTER], U32, name="v_words%d" % n, tag="wt_bf%d" % ((n - 2) * Q // 2), align_bytes=MX_ALIGN)
            quantise_values(words[:], v_planes[n][:], src)
            v_words.append(words[:])

        copies = (nc.scalar.copy, nc.vector.tensor_copy)
        queues = (nc.sync, nc.sync, nc.scalar, nc.sync)
        for n in range(4):
            acc = ps.tile([P, QUARTER], F32, name="acc%d" % n)
            nc.tensor.matmul_mx(
                acc[:], lhsT=w_words[:].bitcast(FP8X4), lhsT_scale=w_plane[:],
                rhs=v_words[n].bitcast(FP8X4), rhs_scale=v_planes[n][:], start=True, stop=True,
            )
            res = sb.tile([P, QUARTER], F32, name="res%d" % n)
            copies[n % 2](res[:], acc[:])
            queues[n].dma_start(out=out[:, n * QUARTER : (n + 1) * QUARTER], in_=res[:])
